import numpy as np
import ml_dtypes


def mxq(x, axis, fmt="e4m3"):
    dtype, down = {"e4m3": (ml_dtypes.float8_e4m3fn, 7), "e5m2": (ml_dtypes.float8_e5m2, 14)}[fmt]
    v = np.moveaxis(np.asarray(x, np.float32).astype(ml_dtypes.bfloat16).astype(np.float64), axis, -1)
    blocks = v.reshape(v.shape[:-1] + (-1, 32))
    amax = np.abs(blocks).max(-1, keepdims=True)
    byte = np.maximum(np.where(amax > 0, np.frexp(amax)[1] - 1 + 127, 0) - down, 1)
    scale = np.exp2(byte - 127.0)
    codes = (blocks / scale).astype(np.float32).astype(dtype).astype(np.float64)
    return np.moveaxis((codes * scale).reshape(v.shape), -1, axis)


WIDE = False


def mx_kscale(k):
    if not WIDE:
        return np.ones(k)
    levels = np.array([10, -10, 5, -5, 0])
    if k % 512:
        return np.exp2(np.random.permutation(np.resize(levels, k // 32))).repeat(32)
    a = np.empty((k // 512, 16))
    for p in range(k // 512):
        a[p, :8] = np.random.permutation(np.resize(levels, 8))
        for g in range(8):
            far = levels[np.abs(levels - a[p, g]) >= 10]
            a[p, g + 8] = far[np.random.randint(len(far))]
    return np.exp2(a.ravel()).repeat(32)


def f64(x):
    return np.asarray(x).astype(np.float64)


def striped(idx):
    return np.tile(idx.reshape(-1, 16).T, (8, 1)).astype(np.uint16)


def unstriped(offs):
    return offs[:16].T.reshape(-1).astype(np.int64)


E2M1 = np.array([0.0, 0.5, 1.0, 1.5, 2.0, 3.0, 4.0, 6.0, -0.0, -0.5, -1.0, -1.5, -2.0, -3.0, -4.0, -6.0])


def pack_weight(w, fmt):
    k, n = w.shape
    w = f64(np.asarray(w, np.float32).astype(ml_dtypes.bfloat16)).reshape(k // 32, 32, n)
    amax = np.abs(w).max(1)
    if fmt == "e4m3":
        byte = np.frexp(amax)[1] - 1 + 127 - 7
    else:
        mant, ex = np.frexp(amax / 6.0)
        byte = np.where(mant > 0.5, ex, ex - 1) + 127
    byte = np.clip(np.where(amax > 0, byte, 1), 1, 254)
    scaled = (w * np.exp2(127.0 - byte)[:, None, :]).reshape(k, n).astype(np.float32)
    by_word = np.ascontiguousarray(scaled.reshape(k // 512, 128, 4, n).transpose(0, 1, 3, 2))
    if fmt == "e4m3":
        words = by_word.astype(ml_dtypes.float8_e4m3fn).view(np.uint8)
    else:
        c = by_word.astype(ml_dtypes.float4_e2m1fn).view(np.uint8) & 0xF
        words = (c[..., 0::2] | (c[..., 1::2] << 4)).reshape(k // 512, 128, 2 * n)
    return np.ascontiguousarray(words), np.ascontiguousarray(byte.astype(np.uint8).reshape(k // 512, 16, n))


def unpack_weight(words, scales, fmt):
    g, _, n = scales.shape
    words = np.ascontiguousarray(words).reshape(g, 128, n, -1)
    if fmt == "e4m3":
        vals = words.view(ml_dtypes.float8_e4m3fn).astype(np.float64)
    else:
        nib = np.empty((g, 128, n, 4), np.uint8)
        nib[..., 0::2] = words & 0xF
        nib[..., 1::2] = words >> 4
        vals = E2M1[nib]
    vals = vals * np.repeat(np.exp2(scales.astype(np.float64) - 127.0), 8, axis=1)[..., None]
    return vals.transpose(0, 1, 3, 2).reshape(g * 512, n)


def gelu(v):
    return 0.5 * v * (1.0 + np.tanh(np.sqrt(2.0 / np.pi) * (v + 0.044715 * v**3)))


K, H, T, S, T2, P = 1024, 1024, 2048, 1024, 2048, 512

def setup_inputs():
    n = np.random.standard_normal
    s = mx_kscale(K)[:, None]
    u = mx_kscale(H)[:, None]
    tab_words, tab_scales = pack_weight(n((K, T)) * s, "e4m3")
    w4_words, w4_scales = pack_weight(0.7 * n((K, H)) / s / np.sqrt(K) * u.T, "e2m1")
    return {
        "tab_words": tab_words, "tab_scales": tab_scales,
        "offs": striped(np.random.permutation(T)[:S]),
        "offs2": striped(np.random.permutation(T2)[:S]),
        "offs3": striped(np.random.permutation(T2)[:P]),
        "offs4": striped(np.random.permutation(T2)[:P]),
        "w1": (1.8 * n((K, H)) / s / np.sqrt(K)).astype(np.float32),
        "w4_words": w4_words, "w4_scales": w4_scales,
        "force": (n((H, S)) * u).astype(np.float32),
        "wgs": np.exp(0.3 * n((128, S))).astype(np.float32),
        "page0": (n((H, T2)) * u).astype(np.float32),
        "chan": (np.random.uniform(0.5, 1.5, H) / u[:, 0] ** 2 / np.sqrt(H)).astype(np.float32),
        "pair": (0.8 * n((P, P))).astype(np.float32),
        "mode": np.exp(0.3 * n(P)).astype(np.float32),
    }

def reference(tab_words, tab_scales, offs, offs2, offs3, offs4, w1, w4_words, w4_scales,
              force, wgs, page0, chan, pair, mode):
    v = unpack_weight(tab_words, tab_scales, "e4m3")[:, unstriped(offs)]
    w4 = unpack_weight(w4_words, w4_scales, "e2m1")
    bend = np.tanh(mxq(f64(w1), 0, "e4m3").T @ v)
    h = f64(force) * bend + (w4.T @ v)
    page = f64(page0).copy()
    page[:, unstriped(offs2)] = np.tile(f64(wgs), (H // 128, 1)) * h
    x1 = page[:, unstriped(offs3)]
    x2 = np.abs(page[:, unstriped(offs4)]) * f64(chan)[:, None]
    e = mxq(x1, 0, "e4m3").T @ mxq(x2, 0, "e4m3")
    return (e + f64(pair)) * f64(mode)[None, :]

@@ -1,0 +1,299 @@
+from contextlib import ExitStack
+
+import concourse.mybir as mybir
+from concourse.masks import make_identity
+
+K, H, T, S, T2, NP = 1024, 1024, 2048, 1024, 2048, 512
+FLOPS = 2 * 2 * K * H * S + 2 * H * NP * NP
+
+F32 = mybir.dt.float32
+BF16 = mybir.dt.bfloat16
+I32 = mybir.dt.int32
+U32 = mybir.dt.uint32
+U16 = mybir.dt.uint16
+U8 = mybir.dt.uint8
+FP8X4 = mybir.dt.float8_e4m3fn_x4
+FP4X4 = mybir.dt.float4_e2m1fn_x4
+MULT = mybir.AluOpType.mult
+ADD = mybir.AluOpType.add
+ACT = mybir.ActivationFunctionType
+
+P = 128
+PACK = 4
+KP = P * PACK
+CUTS = ((0, 256), (256, 256), (512, 512))
+FORCE_CUTS = (CUTS, ((0, 512), (512, 512)))
+STEP = 256
+BIG = 8
+XAT = 6
+
+
+def find(cuts, j):
+    return [i for i, (j0, w) in enumerate(cuts) if j0 <= j < j0 + w][0]
+
+
+def tile_list_bond_mode_scores_kernel(
+    tc, tab_words, tab_scales, offs, offs2, offs3, offs4, w1, w4_words, w4_scales,
+    force, wgs, page0, chan, pair, mode, out,
+):
+    nc = tc.nc
+    with ExitStack() as ctx:
+        keep = ctx.enter_context(tc.tile_pool(name="keep", bufs=1))
+        ring = ctx.enter_context(tc.tile_pool(name="ring", bufs=2))
+        psum = ctx.enter_context(tc.psum_pool(name="psum", bufs=2))
+
+        idx = keep.tile([P, S // 16], U16, name="idx")
+        idx2 = keep.tile([P, S // 16], U16, name="idx2")
+        idx3 = keep.tile([P, NP // 16], U16, name="idx3")
+        idx4 = keep.tile([P, NP // 16], U16, name="idx4")
+
+        tab_s = keep.tile([P, 2, T], U8, name="tab_s", align_bytes=64)
+        w4_s = keep.tile([P, 2, H], U8, name="w4_s", align_bytes=64)
+        nc.gpsimd.memset(tab_s[:, 0, :].bitcast(I32), 0)
+        nc.vector.memset(tab_s[:, 1, :].bitcast(I32), 0)
+        nc.vector.memset(w4_s[:].rearrange("p a n -> p (a n)").bitcast(I32), 0)
+
+        tab_w, w1_raw, w4_w, force_t, page, wg = {}, {}, {}, {}, {}, {}
+
+        def load_tab_scales():
+            for q in range(4):
+                nc.sync.dma_start(
+                    out=tab_s[32 * q : 32 * q + 4, :, :].bitcast(I32),
+                    in_=tab_scales[:, 4 * q : 4 * q + 4, :].rearrange("a r n -> r a n").bitcast(I32),
+                )
+
+        def load_w4_scales():
+            for q in range(4):
+                nc.sync.dma_start(
+                    out=w4_s[32 * q : 32 * q + 4, :, :].bitcast(I32),
+                    in_=w4_scales[:, 4 * q : 4 * q + 4, :].rearrange("a r n -> r a n").bitcast(I32),
+                )
+
+        def load_tab(a):
+            tab_w[a] = ring.tile([P, T], U32, name=f"tab_w{a}", tag="big", bufs=BIG)
+            nc.sync.dma_start(
+                out=tab_w[a][:].bitcast(I32),
+                in_=tab_words[a].rearrange("p n i -> p (n i)").bitcast(I32),
+            )
+
+        def load_w1(a, b):
+            w1_raw[a, b] = ring.tile([P, PACK, KP], F32, name=f"w1_raw{a}{b}", tag="big", bufs=BIG)
+            nc.sync.dma_start(
+                out=w1_raw[a, b][:],
+                in_=w1[KP * a : KP * (a + 1), KP * b : KP * (b + 1)].rearrange("(p i) c -> p i c", i=PACK),
+            )
+
+        def load_w4(b):
+            w4_w[b] = keep.tile([P, 2, 2 * KP], U8, name=f"w4_w{b}", align_bytes=64)
+            nc.sync.dma_start(
+                out=w4_w[b][:].bitcast(I32),
+                in_=w4_words[:, :, 2 * KP * b : 2 * KP * (b + 1)].rearrange("a p n -> p a n").bitcast(I32),
+            )
+
+        def load_force(b, c):
+            j0, w = FORCE_CUTS[b][c]
+            force_t[b, c] = ring.tile([P, PACK, w], F32, name=f"force{b}{c}", tag=f"force_w{w}")
+            nc.sync.dma_start(
+                out=force_t[b, c][:],
+                in_=force[KP * b : KP * (b + 1), j0 : j0 + w].rearrange("(p t) j -> p t j", t=PACK),
+            )
+
+        def load_page(b, t):
+            page[b, t] = ring.tile([P, T2], F32, name=f"page{b}{t}", tag="big", bufs=BIG)
+            nc.sync.dma_start(
+                out=page[b, t][:],
+                in_=page0[KP * b : KP * (b + 1), :].rearrange("(p t) c -> t p c", t=PACK)[t],
+            )
+
+        def load_wgs(c):
+            j0, w = CUTS[c]
+            wg[c] = keep.tile([P, PACK, w], F32, name=f"wg{c}")
+            for q in (0, 2, 1, 3):
+                nc.sync.dma_start(
+                    out=wg[c][32 * q : 32 * (q + 1), :, :],
+                    in_=wgs[:, j0 : j0 + w].rearrange("(p t) j -> p t j", t=PACK),
+                )
+
+        nc.sync.dma_start(idx[:], offs)
+        nc.sync.dma_start(idx2[:], offs2)
+        load_tab_scales()
+        ident = keep.tile([P, P], F32, name="ident")
+        make_identity(nc, ident[:])
+        load_w1(0, 0)
+        load_tab(0)
+        load_w4(0)
+        load_w4_scales()
+        load_w1(1, 0)
+        load_force(0, 0)
+        load_tab(1)
+        load_wgs(0)
+        load_page(0, 0)
+        load_force(0, 1)
+        load_page(0, 1)
+        load_wgs(1)
+        load_force(0, 2)
+        load_page(0, 2)
+        load_page(0, 3)
+        load_w1(0, 1)
+        load_w1(1, 1)
+        load_wgs(2)
+        load_w4(1)
+        load_force(1, 0)
+        load_page(1, 0)
+        nc.sync.dma_start(idx4[:], offs4)
+        nc.sync.dma_start(idx3[:], offs3)
+        chan_t = keep.tile([P, 2, PACK], F32, name="chan_t")
+        nc.sync.dma_start(out=chan_t[:], in_=chan.rearrange("(b p t) -> p b t", b=2, t=PACK))
+        load_force(1, 1)
+        for t in range(1, PACK):
+            load_page(1, t)
+        mode_t = keep.tile([P, NP], F32, name="mode_t")
+        nc.sync.dma_start(out=mode_t[:], in_=mode.partition_broadcast(P))
+        pair_t = ring.tile([P, PACK, NP], F32, name="pair_t", tag="big", bufs=BIG)
+        nc.sync.dma_start(out=pair_t[:], in_=pair.rearrange("(c p) j -> p c j", p=P))
+
+        v_w = [keep.tile([P, S], U32, name=f"v_w{a}", align_bytes=64) for a in range(2)]
+        v_s = [keep.tile([P, S], U8, name=f"v_s{a}", align_bytes=64) for a in range(2)]
+        for a in range(2):
+            nc.vector.tensor_copy(v_s[a][:], tab_s[:, a, :].indirect(idx[:]))
+        nc.vector.tensor_copy(v_w[0][:], tab_w[0][:].indirect(idx[:]))
+
+        w1_q, w1_s = {}, {}
+
+        def quantize_w1(a, b):
+            grouped = ring.tile([P, KP, PACK], BF16, name=f"w1_bf{a}{b}", tag="w1_bf", align_bytes=64)
+            dst = grouped[:].rearrange("p (c n) i -> p c i n", n=4)
+            src = w1_raw[a, b][:].rearrange("p i (c n) -> p c i n", n=4)
+            for half in (slice(0, KP // 8), slice(KP // 8, KP // 4)):
+                nc.scalar.copy(out=dst[:, half], in_=src[:, half])
+            w1_q[a, b] = keep.tile([P, KP], U32, name=f"w1_q{a}{b}", align_bytes=64)
+            w1_s[a, b] = keep.tile([P, KP], U8, name=f"w1_s{a}{b}", align_bytes=64)
+            nc.vector.quantize_mx(
+                out=w1_q[a, b][:].bitcast(FP8X4),
+                scales=w1_s[a, b][:],
+                in_=grouped[:].rearrange("p c i -> p (c i)"),
+            )
+
+        quantize_w1(0, 0)
+        quantize_w1(1, 0)
+        for j0, w in CUTS:
+            nc.vector.tensor_copy(
+                v_w[1][:, j0 : j0 + w], tab_w[1][:].indirect(idx[:, j0 // 16 : (j0 + w) // 16])
+            )
+
+        h, bend, lin = {}, {}, {}
+
+        def products(b, j0):
+            for j in range(j0, j0 + STEP, P):
+                cols = slice(j, j + P)
+                z = psum.tile([P, KP], F32, name="z", tag="z")
+                y = psum.tile([P, KP], F32, name="y", tag="y")
+                for a in range(2):
+                    nc.tensor.matmul_mx(
+                        out=z[:], lhsT=v_w[a][:, cols].bitcast(FP8X4), lhsT_scale=v_s[a][:, cols],
+                        rhs=w1_q[a, b][:].bitcast(FP8X4), rhs_scale=w1_s[a, b][:],
+                        start=(a == 0), stop=(a == 1),
+                    )
+                fc = find(FORCE_CUTS[b], j)
+                fj = j - FORCE_CUTS[b][fc][0]
+                f = psum.tile([P, PACK, P], F32, name="f", tag="f")
+                for t in range(PACK):
+                    nc.tensor.transpose(f[:, t, :], force_t[b, fc][:, t, fj : fj + P], ident[:])
+                for a in range(2):
+                    nc.tensor.matmul_mx(
+                        out=y[:], lhsT=v_w[a][:, cols].bitcast(FP8X4),
+                        lhsT_scale=v_s[a][:, cols],
+                        rhs=w4_w[b][:, a, :].bitcast(FP4X4), rhs_scale=w4_s[:, a, KP * b : KP * (b + 1)],
+                        start=(a == 0), stop=(a == 1),
+                    )
+                bend[b, j] = ring.tile([P, PACK, P], F32, name="bend", tag="bend", bufs=4)
+                lin[b, j] = ring.tile([P, PACK, P], F32, name="lin", tag="lin", bufs=4)
+                nc.scalar.activation(out=bend[b, j][:], in_=z[:].rearrange("p (q t) -> p t q", t=PACK), func=ACT.Tanh)
+                nc.scalar.copy(out=lin[b, j][:], in_=y[:].rearrange("p (q t) -> p t q", t=PACK))
+                nc.vector.tensor_tensor(out=bend[b, j][:], in0=f[:], in1=bend[b, j][:], op=MULT)
+
+        def turn_back(b, j0):
+            c = find(CUTS, j0)
+            if j0 == CUTS[c][0]:
+                h[b, c] = keep.tile([P, PACK, CUTS[c][1]], F32, name=f"h{b}{c}")
+            for j in range(j0, j0 + STEP, P):
+                acc = psum.tile([P, PACK, P], F32, name="acc", tag="acc")
+                for n, part in enumerate((lin[b, j], bend[b, j])):
+                    for t in range(PACK):
+                        nc.tensor.matmul(
+                            acc[:, t, :], lhsT=part[:, t, :], rhs=ident[:], is_transpose=True,
+                            start=(n == 0 and t == 0), stop=(n == 1 and t == PACK - 1),
+                        )
+                hj = j - CUTS[c][0]
+                nc.scalar.copy(out=h[b, c][:, :, hj : hj + P], in_=acc[:])
+
+        x1_rows, x2_rows, x_q, x_s = {}, {}, {}, {}
+
+        def place_and_fetch(b):
+            x1_rows[b] = ring.tile([P, PACK, NP], BF16, name="x1_rows", tag="x1_rows")
+            for c, (j0, w) in enumerate(CUTS):
+                for t in range(PACK):
+                    nc.vector.tensor_tensor(
+                        page[b, t][:].indirect(idx2[:, j0 // 16 : (j0 + w) // 16]),
+                        h[b, c][:, t, :], wg[c][:, t, :], MULT,
+                    )
+                    if c == len(CUTS) - 1:
+                        x2_rows[b, t] = ring.tile([P, NP], F32, name="x2_rows", tag="x2_rows", bufs=5)
+                        nc.vector.tensor_copy(x2_rows[b, t][:], page[b, t][:].indirect(idx4[:]))
+                        nc.vector.tensor_copy(x1_rows[b][:, t, :], page[b, t][:].indirect(idx3[:]))
+
+        def quantize_x(b):
+            x1_g = keep.tile([P, NP, PACK], BF16, name="x1_g", tag="x1_g", align_bytes=64)
+            x2_g = keep.tile([P, NP, PACK], BF16, name="x2_g", tag="x2_g", align_bytes=64)
+            for t in range(PACK):
+                mag = ring.tile([P, NP], F32, name="mag", tag="mag")
+                nc.scalar.activation(out=mag[:], in_=x2_rows[b, t][:], func=ACT.Abs)
+                nc.scalar.activation(out=x2_g[:, :, t], in_=mag[:], func=ACT.Copy, scale=chan_t[:, b, t : t + 1])
+                if t % 2 == 1:
+                    dst = x1_g[:, :, t - 1 : t + 1]
+                    src = x1_rows[b][:, t - 1 : t + 1, :].rearrange("p t m -> p m t")
+                    if b == 1 and t == PACK - 1:
+                        nc.vector.tensor_copy(out=dst, in_=src)
+                    else:
+                        nc.scalar.copy(out=dst, in_=src)
+            for n, grouped in enumerate((x1_g, x2_g)):
+                x_q[n, b] = keep.tile([P, NP], U32, name=f"x_q{n}{b}", align_bytes=64)
+                x_s[n, b] = keep.tile([P, NP], U8, name=f"x_s{n}{b}", align_bytes=64)
+                nc.vector.quantize_mx(
+                    out=x_q[n, b][:].bitcast(FP8X4), scales=x_s[n, b][:],
+                    in_=grouped[:].rearrange("p m t -> p (m t)"),
+                )
+
+        steps = [(b, j0) for b in range(2) for j0 in range(0, S, STEP)]
+        products(*steps[0])
+        turn_back(*steps[0])
+        products(*steps[1])
+        for n in range(2, len(steps)):
+            if steps[n] == (1, 0):
+                turn_back(*steps[n - 1])
+                quantize_w1(0, 1)
+                quantize_w1(1, 1)
+            if n == XAT:
+                place_and_fetch(0)
+                quantize_x(0)
+            products(*steps[n])
+            if steps[n] != (1, 0):
+                turn_back(*steps[n - 1])
+        turn_back(*steps[-1])
+        place_and_fetch(1)
+        quantize_x(1)
+
+        e = [psum.tile([P, NP], F32, name="e", tag=("z", "y")[c % 2]) for c in range(NP // P)]
+        for b in range(2):
+            for c in range(NP // P):
+                cols = slice(c * P, (c + 1) * P)
+                nc.tensor.matmul_mx(
+                    out=e[c][:], lhsT=x_q[0, b][:, cols].bitcast(FP8X4), lhsT_scale=x_s[0, b][:, cols],
+                    rhs=x_q[1, b][:].bitcast(FP8X4), rhs_scale=x_s[1, b][:],
+                    start=(b == 0), stop=(b == 1),
+                )
+        for c in range(NP // P):
+            res = ring.tile([P, NP], F32, name="res", tag="x2_rows", bufs=5)
+            nc.vector.tensor_tensor(out=res[:], in0=e[c][:], in1=pair_t[:, c, :], op=ADD)
+            nc.vector.tensor_tensor(out=res[:], in0=res[:], in1=mode_t[:], op=MULT)
+            nc.sync.dma_start(out=out[c * P : (c + 1) * P, :], in_=res[:])

@@ -1,7 +1,6 @@
 from contextlib import ExitStack
 
 import concourse.mybir as mybir
-from concourse.masks import make_identity
 
 K, H, T, S, T2, NP = 1024, 1024, 2048, 1024, 2048, 512
 FLOPS = 2 * 2 * K * H * S + 2 * H * NP * NP
@@ -21,15 +20,10 @@ ACT = mybir.ActivationFunctionType
 P = 128
 PACK = 4
 KP = P * PACK
-CUTS = ((0, 256), (256, 256), (512, 512))
-FORCE_CUTS = (CUTS, ((0, 512), (512, 512)))
-STEP = 256
-BIG = 8
-XAT = 6
-
-
-def find(cuts, j):
-    return [i for i, (j0, w) in enumerate(cuts) if j0 <= j < j0 + w][0]
+FIRST_CUTS = ((0, 256), (256, 256), (512, 512))
+CUTS = ((0, 512), (512, 512))
+WGS_GROUPS = ((0, 1), (1, 2), (2, 4))
+BIG = 7
 
 
 def tile_list_bond_mode_scores_kernel(
@@ -47,26 +41,27 @@ def tile_list_bond_mode_scores_kernel(
         idx3 = keep.tile([P, NP // 16], U16, name="idx3")
         idx4 = keep.tile([P, NP // 16], U16, name="idx4")
 
-        tab_s = keep.tile([P, 2, T], U8, name="tab_s", align_bytes=64)
-        w4_s = keep.tile([P, 2, H], U8, name="w4_s", align_bytes=64)
-        nc.gpsimd.memset(tab_s[:, 0, :].bitcast(I32), 0)
-        nc.vector.memset(tab_s[:, 1, :].bitcast(I32), 0)
-        nc.vector.memset(w4_s[:].rearrange("p a n -> p (a n)").bitcast(I32), 0)
+        tab_s = keep.tile([P, T], U8, name="tab_s", align_bytes=64)
+        w4_s = keep.tile([P, 2, 2, KP], U8, name="w4_s", align_bytes=64)
+        v_s1 = keep.tile([P, S], U8, name="v_s1", align_bytes=64)
+        nc.gpsimd.memset(tab_s[:].bitcast(I32), 0)
+        nc.vector.memset(w4_s[:].rearrange("p b a n -> p (b a n)").bitcast(I32), 0)
+        nc.vector.memset(v_s1[:].bitcast(I32), 0)
 
         tab_w, w1_raw, w4_w, force_t, page, wg = {}, {}, {}, {}, {}, {}
 
         def load_tab_scales():
             for q in range(4):
                 nc.sync.dma_start(
-                    out=tab_s[32 * q : 32 * q + 4, :, :].bitcast(I32),
-                    in_=tab_scales[:, 4 * q : 4 * q + 4, :].rearrange("a r n -> r a n").bitcast(I32),
+                    out=tab_s[32 * q : 32 * q + 8, :].bitcast(I32),
+                    in_=tab_scales[:, 4 * q : 4 * q + 4, :].bitcast(I32),
                 )
 
-        def load_w4_scales():
+        def load_w4_scales(b):
             for q in range(4):
                 nc.sync.dma_start(
-                    out=w4_s[32 * q : 32 * q + 4, :, :].bitcast(I32),
-                    in_=w4_scales[:, 4 * q : 4 * q + 4, :].rearrange("a r n -> r a n").bitcast(I32),
+                    out=w4_s[32 * q : 32 * q + 4, b].bitcast(I32),
+                    in_=w4_scales[:, 4 * q : 4 * q + 4, KP * b : KP * (b + 1)].rearrange("a r n -> r a n").bitcast(I32),
                 )
 
         def load_tab(a):
@@ -90,12 +85,11 @@ def tile_list_bond_mode_scores_kernel(
                 in_=w4_words[:, :, 2 * KP * b : 2 * KP * (b + 1)].rearrange("a p n -> p a n").bitcast(I32),
             )
 
-        def load_force(b, c):
-            j0, w = FORCE_CUTS[b][c]
-            force_t[b, c] = ring.tile([P, PACK, w], F32, name=f"force{b}{c}", tag=f"force_w{w}")
+        def load_force(b, t):
+            force_t[b, t] = ring.tile([P, S], F32, name=f"force{b}{t}", tag="force", bufs=3)
             nc.sync.dma_start(
-                out=force_t[b, c][:],
-                in_=force[KP * b : KP * (b + 1), j0 : j0 + w].rearrange("(p t) j -> p t j", t=PACK),
+                out=force_t[b, t][:],
+                in_=force[KP * b : KP * (b + 1), :].rearrange("(p t) j -> t p j", t=PACK)[t],
             )
 
         def load_page(b, t):
@@ -105,47 +99,51 @@ def tile_list_bond_mode_scores_kernel(
                 in_=page0[KP * b : KP * (b + 1), :].rearrange("(p t) c -> t p c", t=PACK)[t],
             )
 
-        def load_wgs(c):
-            j0, w = CUTS[c]
-            wg[c] = keep.tile([P, PACK, w], F32, name=f"wg{c}")
+        def load_wgs(g):
+            t0, t1 = WGS_GROUPS[g]
+            rows = keep.tile([P, t1 - t0, S], F32, name=f"wg{g}")
             for q in (0, 2, 1, 3):
                 nc.sync.dma_start(
-                    out=wg[c][32 * q : 32 * (q + 1), :, :],
-                    in_=wgs[:, j0 : j0 + w].rearrange("(p t) j -> p t j", t=PACK),
+                    out=rows[32 * q : 32 * (q + 1), :, :],
+                    in_=wgs.rearrange("(p t) j -> p t j", t=PACK)[:, t0:t1, :],
                 )
+            for t in range(t0, t1):
+                wg[t] = rows[:, t - t0, :]
 
         nc.sync.dma_start(idx[:], offs)
         nc.sync.dma_start(idx2[:], offs2)
         load_tab_scales()
-        ident = keep.tile([P, P], F32, name="ident")
-        make_identity(nc, ident[:])
         load_w1(0, 0)
         load_tab(0)
+        v_s0 = keep.tile([P, S], U8, name="v_s0", align_bytes=64)
+        nc.vector.tensor_copy(v_s0[:], tab_s[:].indirect(idx[:]))
+        nc.sync.dma_start(out=v_s1[0 : P - 4, :].bitcast(I32), in_=v_s0[4:P, :].bitcast(I32))
+        v_s = (v_s0, v_s1)
         load_w4(0)
-        load_w4_scales()
+        load_w4_scales(0)
         load_w1(1, 0)
-        load_force(0, 0)
         load_tab(1)
+        load_force(0, 0)
         load_wgs(0)
         load_page(0, 0)
         load_force(0, 1)
-        load_page(0, 1)
         load_wgs(1)
-        load_force(0, 2)
-        load_page(0, 2)
-        load_page(0, 3)
-        load_w1(0, 1)
-        load_w1(1, 1)
-        load_wgs(2)
-        load_w4(1)
-        load_force(1, 0)
-        load_page(1, 0)
         nc.sync.dma_start(idx4[:], offs4)
         nc.sync.dma_start(idx3[:], offs3)
+        load_page(0, 1)
+        load_force(0, 2)
+        load_wgs(2)
+        load_w1(0, 1)
+        load_w1(1, 1)
+        load_w4(1)
+        load_w4_scales(1)
         chan_t = keep.tile([P, 2, PACK], F32, name="chan_t")
         nc.sync.dma_start(out=chan_t[:], in_=chan.rearrange("(b p t) -> p b t", b=2, t=PACK))
-        load_force(1, 1)
-        for t in range(1, PACK):
+        load_page(0, 2)
+        load_force(0, 3)
+        load_page(0, 3)
+        for t in range(PACK):
+            load_force(1, t)
             load_page(1, t)
         mode_t = keep.tile([P, NP], F32, name="mode_t")
         nc.sync.dma_start(out=mode_t[:], in_=mode.partition_broadcast(P))
@@ -153,98 +151,104 @@ def tile_list_bond_mode_scores_kernel(
         nc.sync.dma_start(out=pair_t[:], in_=pair.rearrange("(c p) j -> p c j", p=P))
 
         v_w = [keep.tile([P, S], U32, name=f"v_w{a}", align_bytes=64) for a in range(2)]
-        v_s = [keep.tile([P, S], U8, name=f"v_s{a}", align_bytes=64) for a in range(2)]
-        for a in range(2):
-            nc.vector.tensor_copy(v_s[a][:], tab_s[:, a, :].indirect(idx[:]))
         nc.vector.tensor_copy(v_w[0][:], tab_w[0][:].indirect(idx[:]))
 
-        w1_q, w1_s = {}, {}
+        w1_q, w1_s, w4_dw, w4_ds = {}, {}, {}, {}
 
         def quantize_w1(a, b):
-            grouped = ring.tile([P, KP, PACK], BF16, name=f"w1_bf{a}{b}", tag="w1_bf", align_bytes=64)
-            dst = grouped[:].rearrange("p (c n) i -> p c i n", n=4)
-            src = w1_raw[a, b][:].rearrange("p i (c n) -> p c i n", n=4)
-            for half in (slice(0, KP // 8), slice(KP // 8, KP // 4)):
-                nc.scalar.copy(out=dst[:, half], in_=src[:, half])
+            grouped = ring.tile([P, PACK, P, PACK], BF16, name=f"w1_bf{a}{b}", tag="w1_bf", align_bytes=64)
+            src = w1_raw[a, b][:].rearrange("p i (m t) -> p t m i", t=PACK)
             w1_q[a, b] = keep.tile([P, KP], U32, name=f"w1_q{a}{b}", align_bytes=64)
             w1_s[a, b] = keep.tile([P, KP], U8, name=f"w1_s{a}{b}", align_bytes=64)
-            nc.vector.quantize_mx(
-                out=w1_q[a, b][:].bitcast(FP8X4),
-                scales=w1_s[a, b][:],
-                in_=grouped[:].rearrange("p c i -> p (c i)"),
+            for u in range(2):
+                nc.scalar.copy(out=grouped[:, 2 * u : 2 * u + 2], in_=src[:, 2 * u : 2 * u + 2])
+            for t0, t1 in ((0, 2), (2, 4)) if (a, b) == (1, 0) else ((0, 4),):
+                nc.vector.quantize_mx(
+                    out=w1_q[a, b][:, P * t0 : P * t1].bitcast(FP8X4),
+                    scales=w1_s[a, b][:, P * t0 : P * t1],
+                    in_=grouped[:, t0:t1].rearrange("p t m i -> p (t m i)"),
+                )
+
+        def deal_w4(b):
+            w4_dw[b] = keep.tile([P, 2, PACK, P, 2], U8, name=f"w4_dw{b}", align_bytes=64)
+            w4_ds[b] = keep.tile([P, 2, PACK, P], U8, name=f"w4_ds{b}", align_bytes=64)
+            nc.vector.tensor_copy(
+                out=w4_dw[b][:], in_=w4_w[b][:].rearrange("p a (m t e) -> p a t m e", t=PACK, e=2)
+            )
+            nc.vector.tensor_copy(
+                out=w4_ds[b][:],
+                in_=w4_s[:, b].rearrange("p a (m t) -> p a t m", t=PACK),
             )
 
         quantize_w1(0, 0)
+        deal_w4(0)
         quantize_w1(1, 0)
-        for j0, w in CUTS:
+        for j0, w in FIRST_CUTS:
             nc.vector.tensor_copy(
                 v_w[1][:, j0 : j0 + w], tab_w[1][:].indirect(idx[:, j0 // 16 : (j0 + w) // 16])
             )
 
-        h, bend, lin = {}, {}, {}
-
-        def products(b, j0):
-            for j in range(j0, j0 + STEP, P):
-                cols = slice(j, j + P)
+        def place(b, t):
+            first = (b, t) == (0, 0)
+            rows = slice(P * t, P * (t + 1))
+            val = ring.tile([P, S], F32, name="val", tag="val", bufs=4, align_bytes=64)
+            add_on_vector = first
+            lin = None if add_on_vector else ring.tile([P, S], F32, name="lin", tag="lin")
+            sums = []
+            for j0, w in FIRST_CUTS if first else CUTS:
+                cols = slice(j0, j0 + w)
                 z = psum.tile([P, KP], F32, name="z", tag="z")
                 y = psum.tile([P, KP], F32, name="y", tag="y")
                 for a in range(2):
                     nc.tensor.matmul_mx(
-                        out=z[:], lhsT=v_w[a][:, cols].bitcast(FP8X4), lhsT_scale=v_s[a][:, cols],
-                        rhs=w1_q[a, b][:].bitcast(FP8X4), rhs_scale=w1_s[a, b][:],
+                        out=z[:, :w], lhsT=w1_q[a, b][:, rows].bitcast(FP8X4), lhsT_scale=w1_s[a, b][:, rows],
+                        rhs=v_w[a][:, cols].bitcast(FP8X4), rhs_scale=v_s[a][:, cols],
                         start=(a == 0), stop=(a == 1),
                     )
-                fc = find(FORCE_CUTS[b], j)
-                fj = j - FORCE_CUTS[b][fc][0]
-                f = psum.tile([P, PACK, P], F32, name="f", tag="f")
-                for t in range(PACK):
-                    nc.tensor.transpose(f[:, t, :], force_t[b, fc][:, t, fj : fj + P], ident[:])
                 for a in range(2):
                     nc.tensor.matmul_mx(
-                        out=y[:], lhsT=v_w[a][:, cols].bitcast(FP8X4),
-                        lhsT_scale=v_s[a][:, cols],
-                        rhs=w4_w[b][:, a, :].bitcast(FP4X4), rhs_scale=w4_s[:, a, KP * b : KP * (b + 1)],
+                        out=y[:, :w], lhsT=w4_dw[b][:, a, t].rearrange("p m e -> p (m e)").bitcast(FP4X4),
+                        lhsT_scale=w4_ds[b][:, a, t, :],
+                        rhs=v_w[a][:, cols].bitcast(FP8X4), rhs_scale=v_s[a][:, cols],
                         start=(a == 0), stop=(a == 1),
                     )
-                bend[b, j] = ring.tile([P, PACK, P], F32, name="bend", tag="bend", bufs=4)
-                lin[b, j] = ring.tile([P, PACK, P], F32, name="lin", tag="lin", bufs=4)
-                nc.scalar.activation(out=bend[b, j][:], in_=z[:].rearrange("p (q t) -> p t q", t=PACK), func=ACT.Tanh)
-                nc.scalar.copy(out=lin[b, j][:], in_=y[:].rearrange("p (q t) -> p t q", t=PACK))
-                nc.vector.tensor_tensor(out=bend[b, j][:], in0=f[:], in1=bend[b, j][:], op=MULT)
-
-        def turn_back(b, j0):
-            c = find(CUTS, j0)
-            if j0 == CUTS[c][0]:
-                h[b, c] = keep.tile([P, PACK, CUTS[c][1]], F32, name=f"h{b}{c}")
-            for j in range(j0, j0 + STEP, P):
-                acc = psum.tile([P, PACK, P], F32, name="acc", tag="acc")
-                for n, part in enumerate((lin[b, j], bend[b, j])):
-                    for t in range(PACK):
-                        nc.tensor.matmul(
-                            acc[:, t, :], lhsT=part[:, t, :], rhs=ident[:], is_transpose=True,
-                            start=(n == 0 and t == 0), stop=(n == 1 and t == PACK - 1),
-                        )
-                hj = j - CUTS[c][0]
-                nc.scalar.copy(out=h[b, c][:, :, hj : hj + P], in_=acc[:])
-
-        x1_rows, x2_rows, x_q, x_s = {}, {}, {}, {}
-
-        def place_and_fetch(b):
-            x1_rows[b] = ring.tile([P, PACK, NP], BF16, name="x1_rows", tag="x1_rows")
-            for c, (j0, w) in enumerate(CUTS):
-                for t in range(PACK):
-                    nc.vector.tensor_tensor(
-                        page[b, t][:].indirect(idx2[:, j0 // 16 : (j0 + w) // 16]),
-                        h[b, c][:, t, :], wg[c][:, t, :], MULT,
+                nc.scalar.activation(out=val[:, cols], in_=z[:, :w], func=ACT.Tanh)
+                if first:
+                    nc.vector.tensor_tensor(out=val[:, cols], in0=val[:, cols], in1=force_t[b, t][:, cols], op=MULT)
+                    nc.vector.tensor_tensor(out=val[:, cols], in0=y[:, :w], in1=val[:, cols], op=ADD)
+                    nc.gpsimd.tensor_tensor(out=val[:, cols], in0=val[:, cols], in1=wg[t][:, cols], op=MULT)
+                    nc.vector.tensor_copy(
+                        page[b, t][:].indirect(idx2[:, j0 // 16 : (j0 + w) // 16]), val[:, cols]
                     )
-                    if c == len(CUTS) - 1:
-                        x2_rows[b, t] = ring.tile([P, NP], F32, name="x2_rows", tag="x2_rows", bufs=5)
-                        nc.vector.tensor_copy(x2_rows[b, t][:], page[b, t][:].indirect(idx4[:]))
-                        nc.vector.tensor_copy(x1_rows[b][:, t, :], page[b, t][:].indirect(idx3[:]))
+                elif add_on_vector:
+                    sums.append((cols, y))
+                else:
+                    nc.scalar.copy(out=lin[:, cols], in_=y[:])
+            if first:
+                return
+            spans = [slice(j0, j0 + w) for j0, w in CUTS]
+            for cols in spans:
+                nc.gpsimd.tensor_tensor(out=val[:, cols], in0=val[:, cols], in1=force_t[b, t][:, cols], op=MULT)
+            for cols, y in sums:
+                nc.vector.tensor_tensor(out=val[:, cols], in0=y[:], in1=val[:, cols], op=ADD)
+            for cols in spans if not add_on_vector else []:
+                nc.gpsimd.tensor_tensor(out=val[:, cols], in0=val[:, cols], in1=lin[:, cols], op=ADD)
+            for cols in spans:
+                nc.gpsimd.tensor_tensor(out=val[:, cols], in0=val[:, cols], in1=wg[t][:, cols], op=MULT)
+            nc.vector.tensor_copy(page[b, t][:].indirect(idx2[:]), val[:])
 
-        def quantize_x(b):
-            x1_g = keep.tile([P, NP, PACK], BF16, name="x1_g", tag="x1_g", align_bytes=64)
-            x2_g = keep.tile([P, NP, PACK], BF16, name="x2_g", tag="x2_g", align_bytes=64)
+        x1_rows, x2_rows, x_g, x_q, x_s = {}, {}, {}, {}, {}
+
+        def fetch(b, t):
+            if t == 0:
+                x1_rows[b] = ring.tile([P, PACK, NP], BF16, name="x1_rows", tag="x1_rows")
+            x2_rows[b, t] = ring.tile([P, NP], F32, name="x2_rows", tag="x2_rows", bufs=5)
+            nc.vector.tensor_copy(x2_rows[b, t][:], page[b, t][:].indirect(idx4[:]))
+            nc.vector.tensor_copy(x1_rows[b][:, t, :], page[b, t][:].indirect(idx3[:]))
+
+        def group_x(b):
+            x1_g = ring.tile([P, NP, PACK], BF16, name="x1_g", tag="x1_g", align_bytes=64)
+            x2_g = ring.tile([P, NP, PACK], BF16, name="x2_g", tag="x2_g", align_bytes=64)
             for t in range(PACK):
                 mag = ring.tile([P, NP], F32, name="mag", tag="mag")
                 nc.scalar.activation(out=mag[:], in_=x2_rows[b, t][:], func=ACT.Abs)
@@ -256,40 +260,39 @@ def tile_list_bond_mode_scores_kernel(
                         nc.vector.tensor_copy(out=dst, in_=src)
                     else:
                         nc.scalar.copy(out=dst, in_=src)
-            for n, grouped in enumerate((x1_g, x2_g)):
-                x_q[n, b] = keep.tile([P, NP], U32, name=f"x_q{n}{b}", align_bytes=64)
+            x_g[b] = (x1_g, x2_g)
+
+        def quantize_x(b):
+            codes = ring.tile([P, 2, NP], U32, name=f"x_q{b}", tag="val", bufs=4, align_bytes=64)
+            for n in range(2):
+                x_q[n, b] = codes[:, n, :]
                 x_s[n, b] = keep.tile([P, NP], U8, name=f"x_s{n}{b}", align_bytes=64)
                 nc.vector.quantize_mx(
-                    out=x_q[n, b][:].bitcast(FP8X4), scales=x_s[n, b][:],
-                    in_=grouped[:].rearrange("p m t -> p (m t)"),
+                    out=x_q[n, b].bitcast(FP8X4), scales=x_s[n, b][:],
+                    in_=x_g[b][n][:].rearrange("p m t -> p (m t)"),
                 )
 
-        steps = [(b, j0) for b in range(2) for j0 in range(0, S, STEP)]
-        products(*steps[0])
-        turn_back(*steps[0])
-        products(*steps[1])
-        for n in range(2, len(steps)):
-            if steps[n] == (1, 0):
-                turn_back(*steps[n - 1])
-                quantize_w1(0, 1)
-                quantize_w1(1, 1)
-            if n == XAT:
-                place_and_fetch(0)
-                quantize_x(0)
-            products(*steps[n])
-            if steps[n] != (1, 0):
-                turn_back(*steps[n - 1])
-        turn_back(*steps[-1])
-        place_and_fetch(1)
+        for b in range(2):
+            for t in range(PACK):
+                if (b, t) == (0, 3):
+                    quantize_w1(0, 1)
+                    quantize_w1(1, 1)
+                    deal_w4(1)
+                if (b, t) == (1, 1):
+                    group_x(0)
+                place(b, t)
+                fetch(b, t)
+        quantize_x(0)
+        group_x(1)
         quantize_x(1)
 
-        e = [psum.tile([P, NP], F32, name="e", tag=("z", "y")[c % 2]) for c in range(NP // P)]
+        e = [psum.tile([P, NP], F32, name=f"e{c}", bufs=1) for c in range(NP // P)]
         for b in range(2):
             for c in range(NP // P):
                 cols = slice(c * P, (c + 1) * P)
                 nc.tensor.matmul_mx(
                     out=e[c][:], lhsT=x_q[0, b][:, cols].bitcast(FP8X4), lhsT_scale=x_s[0, b][:, cols],
-                    rhs=x_q[1, b][:].bitcast(FP8X4), rhs_scale=x_s[1, b][:],
+                    rhs=x_q[1, b].bitcast(FP8X4), rhs_scale=x_s[1, b][:],
                     start=(b == 0), stop=(b == 1),
                 )
         for c in range(NP // P):

@@ -19,11 +19,12 @@ ACT = mybir.ActivationFunctionType
 
 P = 128
 PACK = 4
+RUN = 2
 KP = P * PACK
-FIRST_CUTS = ((0, 256), (256, 256), (512, 512))
-CUTS = ((0, 512), (512, 512))
-WGS_GROUPS = ((0, 1), (1, 2), (2, 4))
-BIG = 7
+HALVES = (slice(0, 512), slice(512, 1024))
+WHOLE = slice(0, S)
+NSLICE = H // P
+PAGE_SLOT = (4, 5, 6, 4, 5, 6, 4, 5)
 
 
 def tile_list_bond_mode_scores_kernel(
@@ -34,269 +35,317 @@ def tile_list_bond_mode_scores_kernel(
     with ExitStack() as ctx:
         keep = ctx.enter_context(tc.tile_pool(name="keep", bufs=1))
         ring = ctx.enter_context(tc.tile_pool(name="ring", bufs=2))
-        psum = ctx.enter_context(tc.psum_pool(name="psum", bufs=2))
+        psum = ctx.enter_context(tc.psum_pool(name="psum", bufs=4))
+
+        def in_slot(slot, shape, dtype, name):
+            return keep.tile(shape, dtype, name=name, tag=f"slot{slot}", align_bytes=64)
+
+        def slice_rows(mat, s):
+            b, t = divmod(s, PACK)
+            return mat[KP * b : KP * (b + 1), :].rearrange("(g t u) j -> t g u j", t=PACK, u=RUN)[t]
 
         idx = keep.tile([P, S // 16], U16, name="idx")
         idx2 = keep.tile([P, S // 16], U16, name="idx2")
         idx3 = keep.tile([P, NP // 16], U16, name="idx3")
         idx4 = keep.tile([P, NP // 16], U16, name="idx4")
 
-        tab_s = keep.tile([P, T], U8, name="tab_s", align_bytes=64)
-        w4_s = keep.tile([P, 2, 2, KP], U8, name="w4_s", align_bytes=64)
-        v_s1 = keep.tile([P, S], U8, name="v_s1", align_bytes=64)
-        nc.gpsimd.memset(tab_s[:].bitcast(I32), 0)
-        nc.vector.memset(w4_s[:].rearrange("p b a n -> p (b a n)").bitcast(I32), 0)
-        nc.vector.memset(v_s1[:].bitcast(I32), 0)
+        tab_s = keep.tile([P, 2, T], U8, name="tab_s", align_bytes=64)
+        w4_s = keep.tile([P, 2, H], U8, name="w4_s", align_bytes=64)
+        nc.gpsimd.memset(tab_s[:, 0, :].bitcast(I32), 0)
+        nc.vector.memset(tab_s[:, 1, :].bitcast(I32), 0)
+        nc.vector.memset(w4_s[:].rearrange("p a n -> p (a n)").bitcast(I32), 0)
 
-        tab_w, w1_raw, w4_w, force_t, page, wg = {}, {}, {}, {}, {}, {}
+        tab_w, w1_raw, w4_w, force_t, page, wg, chan_t = {}, {}, {}, {}, {}, {}, {}
 
-        def load_tab_scales():
+        def load_scales(plane, scales):
             for q in range(4):
                 nc.sync.dma_start(
-                    out=tab_s[32 * q : 32 * q + 8, :].bitcast(I32),
-                    in_=tab_scales[:, 4 * q : 4 * q + 4, :].bitcast(I32),
-                )
-
-        def load_w4_scales(b):
-            for q in range(4):
-                nc.sync.dma_start(
-                    out=w4_s[32 * q : 32 * q + 4, b].bitcast(I32),
-                    in_=w4_scales[:, 4 * q : 4 * q + 4, KP * b : KP * (b + 1)].rearrange("a r n -> r a n").bitcast(I32),
+                    out=plane[32 * q : 32 * q + 4, :, :].bitcast(I32),
+                    in_=scales[:, 4 * q : 4 * q + 4, :].rearrange("a r n -> r a n").bitcast(I32),
                 )
 
         def load_tab(a):
-            tab_w[a] = ring.tile([P, T], U32, name=f"tab_w{a}", tag="big", bufs=BIG)
+            tab_w[a] = in_slot(2 * a, [P, T], U32, f"tab_w{a}")
             nc.sync.dma_start(
                 out=tab_w[a][:].bitcast(I32),
                 in_=tab_words[a].rearrange("p n i -> p (n i)").bitcast(I32),
             )
 
         def load_w1(a, b):
-            w1_raw[a, b] = ring.tile([P, PACK, KP], F32, name=f"w1_raw{a}{b}", tag="big", bufs=BIG)
+            w1_raw[a, b] = in_slot((2 * a + 1, 7 + a)[b], [P, PACK, KP], F32, f"w1_raw{a}{b}")
             nc.sync.dma_start(
                 out=w1_raw[a, b][:],
                 in_=w1[KP * a : KP * (a + 1), KP * b : KP * (b + 1)].rearrange("(p i) c -> p i c", i=PACK),
             )
 
         def load_w4(b):
-            w4_w[b] = keep.tile([P, 2, 2 * KP], U8, name=f"w4_w{b}", align_bytes=64)
+            w4_w[b] = keep.tile([P, 2, KP // 2], I32, name=f"w4_w{b}")
             nc.sync.dma_start(
-                out=w4_w[b][:].bitcast(I32),
+                out=w4_w[b][:],
                 in_=w4_words[:, :, 2 * KP * b : 2 * KP * (b + 1)].rearrange("a p n -> p a n").bitcast(I32),
             )
 
-        def load_force(b, t):
-            force_t[b, t] = ring.tile([P, S], F32, name=f"force{b}{t}", tag="force", bufs=3)
-            nc.sync.dma_start(
-                out=force_t[b, t][:],
-                in_=force[KP * b : KP * (b + 1), :].rearrange("(p t) j -> t p j", t=PACK)[t],
-            )
+        def load_force(s):
+            force_t[s] = keep.tile([P, S], F32, name=f"force{s}")
+            nc.sync.dma_start(out=force_t[s][:], in_=slice_rows(force, s))
 
-        def load_page(b, t):
-            page[b, t] = ring.tile([P, T2], F32, name=f"page{b}{t}", tag="big", bufs=BIG)
-            nc.sync.dma_start(
-                out=page[b, t][:],
-                in_=page0[KP * b : KP * (b + 1), :].rearrange("(p t) c -> t p c", t=PACK)[t],
-            )
+        def load_page(s):
+            page[s] = in_slot(PAGE_SLOT[s], [P, T2], F32, f"page{s}")
+            nc.sync.dma_start(out=page[s][:], in_=slice_rows(page0, s))
 
-        def load_wgs(g):
-            t0, t1 = WGS_GROUPS[g]
-            rows = keep.tile([P, t1 - t0, S], F32, name=f"wg{g}")
+        def load_wgs(t):
+            wg[t] = keep.tile([P, S], F32, name=f"wg{t}")
             for q in (0, 2, 1, 3):
                 nc.sync.dma_start(
-                    out=rows[32 * q : 32 * (q + 1), :, :],
-                    in_=wgs.rearrange("(p t) j -> p t j", t=PACK)[:, t0:t1, :],
+                    out=wg[t][32 * q : 32 * (q + 1), :],
+                    in_=wgs.rearrange("(g t u) j -> t g u j", t=PACK, u=RUN)[t],
                 )
-            for t in range(t0, t1):
-                wg[t] = rows[:, t - t0, :]
+
+        def load_chan(s):
+            chan_t[s] = keep.tile([P, 1], F32, name=f"chan{s}")
+            with nc.allow_non_contiguous_dma(reason="one value a partition"):
+                nc.sync.dma_start(out=chan_t[s][:], in_=slice_rows(chan.unsqueeze(1), s))
 
         nc.sync.dma_start(idx[:], offs)
-        nc.sync.dma_start(idx2[:], offs2)
-        load_tab_scales()
+        load_w4(0)
+        load_scales(tab_s, tab_scales)
         load_w1(0, 0)
         load_tab(0)
-        v_s0 = keep.tile([P, S], U8, name="v_s0", align_bytes=64)
-        nc.vector.tensor_copy(v_s0[:], tab_s[:].indirect(idx[:]))
-        nc.sync.dma_start(out=v_s1[0 : P - 4, :].bitcast(I32), in_=v_s0[4:P, :].bitcast(I32))
-        v_s = (v_s0, v_s1)
-        load_w4(0)
-        load_w4_scales(0)
+        load_scales(w4_s, w4_scales)
         load_w1(1, 0)
         load_tab(1)
-        load_force(0, 0)
+        nc.sync.dma_start(idx2[:], offs2)
+        force_first = []
+        for c, cols in enumerate(HALVES):
+            force_first.append(keep.tile([P, KP], F32, name=f"force_first{c}", tag=f"first{c}", align_bytes=64))
+            nc.sync.dma_start(out=force_first[c][:], in_=slice_rows(force[:, cols], 0))
+        load_force(1)
         load_wgs(0)
-        load_page(0, 0)
-        load_force(0, 1)
-        load_wgs(1)
+        load_force(2)
+        load_page(0)
         nc.sync.dma_start(idx4[:], offs4)
         nc.sync.dma_start(idx3[:], offs3)
-        load_page(0, 1)
-        load_force(0, 2)
-        load_wgs(2)
+        load_wgs(1)
         load_w1(0, 1)
+        load_chan(0)
         load_w1(1, 1)
+        load_chan(1)
+        load_force(3)
+        load_wgs(2)
+        load_page(1)
         load_w4(1)
-        load_w4_scales(1)
-        chan_t = keep.tile([P, 2, PACK], F32, name="chan_t")
-        nc.sync.dma_start(out=chan_t[:], in_=chan.rearrange("(b p t) -> p b t", b=2, t=PACK))
-        load_page(0, 2)
-        load_force(0, 3)
-        load_page(0, 3)
-        for t in range(PACK):
-            load_force(1, t)
-            load_page(1, t)
+        load_force(4)
+        load_wgs(3)
+        load_page(2)
+        for s in range(5, NSLICE):
+            load_chan(s - 3)
+            load_force(s)
+        for s in range(5, NSLICE):
+            load_chan(s)
         mode_t = keep.tile([P, NP], F32, name="mode_t")
         nc.sync.dma_start(out=mode_t[:], in_=mode.partition_broadcast(P))
-        pair_t = ring.tile([P, PACK, NP], F32, name="pair_t", tag="big", bufs=BIG)
+        pair_t = in_slot(3, [P, PACK, NP], F32, "pair_t")
         nc.sync.dma_start(out=pair_t[:], in_=pair.rearrange("(c p) j -> p c j", p=P))
 
         v_w = [keep.tile([P, S], U32, name=f"v_w{a}", align_bytes=64) for a in range(2)]
+        v_s = [keep.tile([P, S], U8, name=f"v_s{a}", align_bytes=64) for a in range(2)]
+        for a in range(2):
+            nc.vector.tensor_copy(v_s[a][:], tab_s[:, a, :].indirect(idx[:]))
         nc.vector.tensor_copy(v_w[0][:], tab_w[0][:].indirect(idx[:]))
 
-        w1_q, w1_s, w4_dw, w4_ds = {}, {}, {}, {}
+        w4_dw, w4_ds = {}, {}
 
-        def quantize_w1(a, b):
-            grouped = ring.tile([P, PACK, P, PACK], BF16, name=f"w1_bf{a}{b}", tag="w1_bf", align_bytes=64)
-            src = w1_raw[a, b][:].rearrange("p i (m t) -> p t m i", t=PACK)
-            w1_q[a, b] = keep.tile([P, KP], U32, name=f"w1_q{a}{b}", align_bytes=64)
-            w1_s[a, b] = keep.tile([P, KP], U8, name=f"w1_s{a}{b}", align_bytes=64)
-            for u in range(2):
-                nc.scalar.copy(out=grouped[:, 2 * u : 2 * u + 2], in_=src[:, 2 * u : 2 * u + 2])
-            for t0, t1 in ((0, 2), (2, 4)) if (a, b) == (1, 0) else ((0, 4),):
-                nc.vector.quantize_mx(
-                    out=w1_q[a, b][:, P * t0 : P * t1].bitcast(FP8X4),
-                    scales=w1_s[a, b][:, P * t0 : P * t1],
-                    in_=grouped[:, t0:t1].rearrange("p t m i -> p (t m i)"),
-                )
+        def deal_w4_words(b):
+            w4_dw[b] = keep.tile([P, 2, PACK, 2 * P], U8, name=f"w4_dw{b}", tag=("w4_dw0", "cast3")[b], align_bytes=64)
+            nc.vector.tensor_copy(out=w4_dw[b][:].bitcast(I32), in_=w4_w[b][:].rearrange("p a (g t) -> p a t g", t=PACK))
 
-        def deal_w4(b):
-            w4_dw[b] = keep.tile([P, 2, PACK, P, 2], U8, name=f"w4_dw{b}", align_bytes=64)
-            w4_ds[b] = keep.tile([P, 2, PACK, P], U8, name=f"w4_ds{b}", align_bytes=64)
+        def deal_w4_scales(b):
+            w4_ds[b] = keep.tile([P, 2, PACK, P], U8, name=f"w4_ds{b}", tag=("w4_ds0", "cast2")[b], align_bytes=64)
             nc.vector.tensor_copy(
-                out=w4_dw[b][:], in_=w4_w[b][:].rearrange("p a (m t e) -> p a t m e", t=PACK, e=2)
-            )
-            nc.vector.tensor_copy(
-                out=w4_ds[b][:],
-                in_=w4_s[:, b].rearrange("p a (m t) -> p a t m", t=PACK),
+                out=w4_ds[b][:].rearrange("p a t (g u) -> p a t g u", u=RUN),
+                in_=w4_s[:, :, KP * b : KP * (b + 1)].rearrange("p a (g t u) -> p a t g u", t=PACK, u=RUN),
             )
 
-        quantize_w1(0, 0)
-        deal_w4(0)
-        quantize_w1(1, 0)
-        for j0, w in FIRST_CUTS:
-            nc.vector.tensor_copy(
-                v_w[1][:, j0 : j0 + w], tab_w[1][:].indirect(idx[:, j0 // 16 : (j0 + w) // 16])
+        w1_q = {}
+        w1_s = [keep.tile([P, 2 * KP], U8, name=f"w1_s{b}", align_bytes=64) for b in range(2)]
+
+        def quantize_w1(b, g0, g1, tag):
+            grouped = keep.tile([P, g1 - g0, P // RUN, RUN, PACK], BF16, name=f"w1_bf{b}{g0}", tag=tag, align_bytes=64)
+            if g0 == 0:
+                w1_q[b] = keep.tile([P, 2 * KP], U32, name=f"w1_q{b}", tag=("w1_q0", "placed1")[b], align_bytes=64)
+            step = 2
+            for g in range(g0, g1, step):
+                a, t = divmod(g, PACK)
+                src = w1_raw[a, b][:].rearrange("p i (g t u) -> p t g u i", t=PACK, u=RUN)
+                nc.scalar.copy(out=grouped[:, g - g0 : g - g0 + step], in_=src[:, t : t + step])
+            nc.vector.quantize_mx(
+                out=w1_q[b][:, P * g0 : P * g1].bitcast(FP8X4),
+                scales=w1_s[b][:, P * g0 : P * g1],
+                in_=grouped[:].rearrange("p n g u i -> p (n g u i)"),
             )
 
-        def place(b, t):
-            first = (b, t) == (0, 0)
-            rows = slice(P * t, P * (t + 1))
-            val = ring.tile([P, S], F32, name="val", tag="val", bufs=4, align_bytes=64)
-            add_on_vector = first
-            lin = None if add_on_vector else ring.tile([P, S], F32, name="lin", tag="lin")
-            sums = []
-            for j0, w in FIRST_CUTS if first else CUTS:
-                cols = slice(j0, j0 + w)
+        def gather_words(a, cols):
+            nc.vector.tensor_copy(v_w[a][:, cols], tab_w[a][:].indirect(idx[:, cols.start // 16 : cols.stop // 16]))
+
+        deal_w4_words(0)
+        deal_w4_scales(0)
+        quantize_w1(0, 0, 4, "cast0")
+        quantize_w1(0, 4, 6, "cast1")
+        for cols in HALVES:
+            gather_words(1, cols)
+        quantize_w1(0, 6, 8, "cast1")
+
+        bend, lin, lin_sb, prod, feat, placed = {}, {}, {}, {}, {}, {}
+
+        def products(s):
+            b, t = divmod(s, PACK)
+            bend[s] = keep.tile([P, S], F32, name=f"bend{s}", tag=f"bend{s % 4}", align_bytes=64)
+            for c, cols in enumerate(HALVES):
                 z = psum.tile([P, KP], F32, name="z", tag="z")
-                y = psum.tile([P, KP], F32, name="y", tag="y")
+                lin[s, c] = psum.tile([P, KP], F32, name="y", tag="y")
                 for a in range(2):
+                    rows = slice(KP * a + P * t, KP * a + P * (t + 1))
                     nc.tensor.matmul_mx(
-                        out=z[:, :w], lhsT=w1_q[a, b][:, rows].bitcast(FP8X4), lhsT_scale=w1_s[a, b][:, rows],
+                        out=z[:], lhsT=w1_q[b][:, rows].bitcast(FP8X4), lhsT_scale=w1_s[b][:, rows],
                         rhs=v_w[a][:, cols].bitcast(FP8X4), rhs_scale=v_s[a][:, cols],
                         start=(a == 0), stop=(a == 1),
                     )
                 for a in range(2):
                     nc.tensor.matmul_mx(
-                        out=y[:, :w], lhsT=w4_dw[b][:, a, t].rearrange("p m e -> p (m e)").bitcast(FP4X4),
+                        out=lin[s, c][:], lhsT=w4_dw[b][:, a, t, :].bitcast(FP4X4),
                         lhsT_scale=w4_ds[b][:, a, t, :],
                         rhs=v_w[a][:, cols].bitcast(FP8X4), rhs_scale=v_s[a][:, cols],
                         start=(a == 0), stop=(a == 1),
                     )
-                nc.scalar.activation(out=val[:, cols], in_=z[:, :w], func=ACT.Tanh)
-                if first:
-                    nc.vector.tensor_tensor(out=val[:, cols], in0=val[:, cols], in1=force_t[b, t][:, cols], op=MULT)
-                    nc.vector.tensor_tensor(out=val[:, cols], in0=y[:, :w], in1=val[:, cols], op=ADD)
-                    nc.gpsimd.tensor_tensor(out=val[:, cols], in0=val[:, cols], in1=wg[t][:, cols], op=MULT)
-                    nc.vector.tensor_copy(
-                        page[b, t][:].indirect(idx2[:, j0 // 16 : (j0 + w) // 16]), val[:, cols]
-                    )
-                elif add_on_vector:
-                    sums.append((cols, y))
-                else:
-                    nc.scalar.copy(out=lin[:, cols], in_=y[:])
-            if first:
-                return
-            spans = [slice(j0, j0 + w) for j0, w in CUTS]
-            for cols in spans:
-                nc.gpsimd.tensor_tensor(out=val[:, cols], in0=val[:, cols], in1=force_t[b, t][:, cols], op=MULT)
-            for cols, y in sums:
-                nc.vector.tensor_tensor(out=val[:, cols], in0=y[:], in1=val[:, cols], op=ADD)
-            for cols in spans if not add_on_vector else []:
-                nc.gpsimd.tensor_tensor(out=val[:, cols], in0=val[:, cols], in1=lin[:, cols], op=ADD)
-            for cols in spans:
-                nc.gpsimd.tensor_tensor(out=val[:, cols], in0=val[:, cols], in1=wg[t][:, cols], op=MULT)
-            nc.vector.tensor_copy(page[b, t][:].indirect(idx2[:]), val[:])
+                nc.scalar.activation(out=bend[s][:, cols], in_=z[:], func=ACT.Tanh)
+            if s > 2:
+                copy_linear(s)
+
+        def copy_linear(s):
+            if s == 2:
+                lin_sb[s] = keep.tile([P, KP], F32, name="lin_sb2", tag="feat1", align_bytes=64)
+            else:
+                lin_sb[s] = ring.tile([P, KP], F32, name="lin_sb", tag="lin_sb")
+            nc.scalar.copy(out=lin_sb[s][:], in_=lin[s, 1][:])
+
+        def times_force(s, cols):
+            if s not in prod:
+                prod[s] = ring.tile([P, S], F32, name="prod", tag="prod", bufs=1)
+            nc.gpsimd.tensor_tensor(out=prod[s][:, cols], in0=bend[s][:, cols], in1=force_t[s][:, cols], op=MULT)
+
+        def add_linear(s):
+            tag = {2: "feat0", 3: "cast4"}.get(s, f"bend{(s - 1) % 4}")
+            low = keep.tile([P, KP], F32, name=f"feat_low{s}", tag=tag, align_bytes=64)
+            nc.vector.tensor_tensor(out=low[:], in0=lin[s, 0][:], in1=prod[s][:, HALVES[0]], op=ADD)
+            high = in_slot(PAGE_SLOT[s - 2], [P, KP], F32, f"feat_high{s}")
+            nc.gpsimd.tensor_tensor(out=high[:], in0=prod[s][:, HALVES[1]], in1=lin_sb[s][:], op=ADD)
+            feat[s] = (low, high)
+
+        def weigh(s):
+            placed[s] = keep.tile([P, S], F32, name=f"placed{s}", tag=f"bend{(s + 1) % 4}", align_bytes=64)
+            for part, cols in zip(feat[s], HALVES):
+                nc.gpsimd.tensor_tensor(out=placed[s][:, cols], in0=part[:], in1=wg[s % PACK][:, cols], op=MULT)
+
+        def scatter(s, cols, values):
+            entries = idx2[:, cols.start // 16 : cols.stop // 16]
+            nc.vector.tensor_copy(page[s][:].indirect(entries), values)
 
         x1_rows, x2_rows, x_g, x_q, x_s = {}, {}, {}, {}, {}
 
-        def fetch(b, t):
+        def fetch(s):
+            b, t = divmod(s, PACK)
             if t == 0:
                 x1_rows[b] = ring.tile([P, PACK, NP], BF16, name="x1_rows", tag="x1_rows")
-            x2_rows[b, t] = ring.tile([P, NP], F32, name="x2_rows", tag="x2_rows", bufs=5)
-            nc.vector.tensor_copy(x2_rows[b, t][:], page[b, t][:].indirect(idx4[:]))
-            nc.vector.tensor_copy(x1_rows[b][:, t, :], page[b, t][:].indirect(idx3[:]))
+            x2_rows[s] = ring.tile([P, NP], F32, name="x2_rows", tag="x2_rows", bufs=5)
+            nc.vector.tensor_copy(x2_rows[s][:], page[s][:].indirect(idx4[:]))
+            nc.vector.tensor_copy(x1_rows[b][:, t, :], page[s][:].indirect(idx3[:]))
 
         def group_x(b):
-            x1_g = ring.tile([P, NP, PACK], BF16, name="x1_g", tag="x1_g", align_bytes=64)
-            x2_g = ring.tile([P, NP, PACK], BF16, name="x2_g", tag="x2_g", align_bytes=64)
+            x_g[b] = in_slot(8 - b, [P, 2, NP, PACK], BF16, f"x_g{b}")
+            x1_g, x2_g = x_g[b][:, 0], x_g[b][:, 1]
             for t in range(PACK):
-                mag = ring.tile([P, NP], F32, name="mag", tag="mag")
-                nc.scalar.activation(out=mag[:], in_=x2_rows[b, t][:], func=ACT.Abs)
-                nc.scalar.activation(out=x2_g[:, :, t], in_=mag[:], func=ACT.Copy, scale=chan_t[:, b, t : t + 1])
+                s = PACK * b + t
+                if b == 0:
+                    mag = in_slot(7, [P, NP], F32, "mag")
+                else:
+                    mag = keep.tile([P, NP], F32, name="mag", tag="mag")
+                nc.scalar.activation(out=mag[:], in_=x2_rows[s][:], func=ACT.Abs)
+                nc.scalar.activation(out=x2_g[:, :, t], in_=mag[:], func=ACT.Copy, scale=chan_t[s][:])
                 if t % 2 == 1:
                     dst = x1_g[:, :, t - 1 : t + 1]
                     src = x1_rows[b][:, t - 1 : t + 1, :].rearrange("p t m -> p m t")
-                    if b == 1 and t == PACK - 1:
+                    if s == NSLICE - 1:
                         nc.vector.tensor_copy(out=dst, in_=src)
                     else:
                         nc.scalar.copy(out=dst, in_=src)
-            x_g[b] = (x1_g, x2_g)
 
-        def quantize_x(b):
-            codes = ring.tile([P, 2, NP], U32, name=f"x_q{b}", tag="val", bufs=4, align_bytes=64)
-            for n in range(2):
-                x_q[n, b] = codes[:, n, :]
-                x_s[n, b] = keep.tile([P, NP], U8, name=f"x_s{n}{b}", align_bytes=64)
+        def quantize_x(b, pieces):
+            x_q[b] = keep.tile([P, 2 * NP], U32, name=f"x_q{b}", tag=f"bend{3 - b}", align_bytes=64)
+            x_s[b] = keep.tile([P, 2 * NP], U8, name=f"x_s{b}", align_bytes=64)
+            for n0, n1 in pieces:
                 nc.vector.quantize_mx(
-                    out=x_q[n, b].bitcast(FP8X4), scales=x_s[n, b][:],
-                    in_=x_g[b][n][:].rearrange("p m t -> p (m t)"),
+                    out=x_q[b][:, NP * n0 : NP * n1].bitcast(FP8X4), scales=x_s[b][:, NP * n0 : NP * n1],
+                    in_=x_g[b][:, n0:n1].rearrange("p n m t -> p (n m t)"),
                 )
 
-        for b in range(2):
-            for t in range(PACK):
-                if (b, t) == (0, 3):
-                    quantize_w1(0, 1)
-                    quantize_w1(1, 1)
-                    deal_w4(1)
-                if (b, t) == (1, 1):
-                    group_x(0)
-                place(b, t)
-                fetch(b, t)
-        quantize_x(0)
+        products(0)
+        first = [keep.tile([P, KP], F32, name=f"first_feat{c}", tag=f"feat{1 - c}", align_bytes=64) for c in range(2)]
+        for c, cols in enumerate(HALVES):
+            nc.vector.tensor_tensor(out=bend[0][:, cols], in0=bend[0][:, cols], in1=force_first[c][:], op=MULT)
+        for c, cols in enumerate(HALVES):
+            nc.vector.tensor_tensor(out=first[c][:], in0=lin[0, c][:], in1=bend[0][:, cols], op=ADD)
+            engine = (nc.vector, nc.gpsimd)[c]
+            engine.tensor_tensor(out=first[c][:], in0=first[c][:], in1=wg[0][:, cols], op=MULT)
+        products(1)
+        prod[1] = bend[1]
+        for cols in HALVES:
+            times_force(1, cols)
+        scatter(0, HALVES[0], first[0][:])
+        second = keep.tile([P, S], F32, name="second_feat", tag="feat1", align_bytes=64)
+        for c, cols in enumerate(HALVES):
+            nc.vector.tensor_tensor(out=second[:, cols], in0=lin[1, c][:], in1=bend[1][:, cols], op=ADD)
+        scatter(0, HALVES[1], first[1][:])
+        products(2)
+        times_force(2, WHOLE)
+        placed[1] = keep.tile([P, S], F32, name="placed1", align_bytes=64)
+        nc.gpsimd.tensor_tensor(out=placed[1][:], in0=second[:], in1=wg[1][:], op=MULT)
+        copy_linear(2)
+        fetch(0)
+        for s in range(1, NSLICE):
+            if s + 1 < NSLICE:
+                add_linear(s + 1)
+            if s + 2 < NSLICE:
+                products(s + 2)
+                times_force(s + 2, WHOLE)
+            if s + 1 < NSLICE:
+                weigh(s + 1)
+            if s + 2 < NSLICE:
+                load_page(s + 2)
+            scatter(s, WHOLE, placed[s][:])
+            if s == 1:
+                quantize_w1(1, 0, 4, "cast2")
+                quantize_w1(1, 4, 6, "cast3")
+                quantize_w1(1, 6, 8, "cast4")
+                deal_w4_words(1)
+                deal_w4_scales(1)
+            fetch(s)
+        group_x(0)
+        quantize_x(0, ((0, 2),))
         group_x(1)
-        quantize_x(1)
+        quantize_x(1, ((0, 1), (1, 2)))
 
-        e = [psum.tile([P, NP], F32, name=f"e{c}", bufs=1) for c in range(NP // P)]
+        e = [psum.tile([P, NP], F32, name="e", tag="z") for c in range(NP // P)]
         for b in range(2):
             for c in range(NP // P):
                 cols = slice(c * P, (c + 1) * P)
                 nc.tensor.matmul_mx(
-                    out=e[c][:], lhsT=x_q[0, b][:, cols].bitcast(FP8X4), lhsT_scale=x_s[0, b][:, cols],
-                    rhs=x_q[1, b].bitcast(FP8X4), rhs_scale=x_s[1, b][:],
+                    out=e[c][:], lhsT=x_q[b][:, cols].bitcast(FP8X4), lhsT_scale=x_s[b][:, cols],
+                    rhs=x_q[b][:, NP:].bitcast(FP8X4), rhs_scale=x_s[b][:, NP:],
                     start=(b == 0), stop=(b == 1),
                 )
         for c in range(NP // P):
             res = ring.tile([P, NP], F32, name="res", tag="x2_rows", bufs=5)
             nc.vector.tensor_tensor(out=res[:], in0=e[c][:], in1=pair_t[:, c, :], op=ADD)
-            nc.vector.tensor_tensor(out=res[:], in0=res[:], in1=mode_t[:], op=MULT)
+            engine = nc.gpsimd if c == 0 else nc.vector
+            engine.tensor_tensor(out=res[:], in0=res[:], in1=mode_t[:], op=MULT)
             nc.sync.dma_start(out=out[c * P : (c + 1) * P, :], in_=res[:])

@@ -21,10 +21,13 @@ P = 128
 PACK = 4
 RUN = 2
 KP = P * PACK
-HALVES = (slice(0, 512), slice(512, 1024))
-WHOLE = slice(0, S)
 NSLICE = H // P
-PAGE_SLOT = (4, 5, 6, 4, 5, 6, 4, 5)
+HALVES = (slice(0, KP), slice(KP, S))
+WHOLE = slice(0, S)
+PAGE_BUFS = 4
+WORK_BUFS = 4
+LOW_BUFFER = {2: "first_buf1", 3: "cast_b3"}
+X2_BUFS = 5
 
 
 def tile_list_bond_mode_scores_kernel(
@@ -37,12 +40,21 @@ def tile_list_bond_mode_scores_kernel(
         ring = ctx.enter_context(tc.tile_pool(name="ring", bufs=2))
         psum = ctx.enter_context(tc.psum_pool(name="psum", bufs=4))
 
-        def in_slot(slot, shape, dtype, name):
-            return keep.tile(shape, dtype, name=name, tag=f"slot{slot}", align_bytes=64)
+        def on_buffer(tag, shape, dtype, name):
+            return keep.tile(shape, dtype, name=name, tag=tag, align_bytes=64)
+
+        def page_buffer(s):
+            return f"page_buf{s % PAGE_BUFS}"
+
+        def work_buffer(n):
+            return f"work_buf{n % WORK_BUFS}"
 
         def slice_rows(mat, s):
             b, t = divmod(s, PACK)
             return mat[KP * b : KP * (b + 1), :].rearrange("(g t u) j -> t g u j", t=PACK, u=RUN)[t]
+
+        def entries(offsets, cols):
+            return offsets[:, cols.start // 16 : cols.stop // 16]
 
         idx = keep.tile([P, S // 16], U16, name="idx")
         idx2 = keep.tile([P, S // 16], U16, name="idx2")
@@ -57,29 +69,29 @@ def tile_list_bond_mode_scores_kernel(
 
         tab_w, w1_raw, w4_w, force_t, page, wg, chan_t = {}, {}, {}, {}, {}, {}, {}
 
-        def load_scales(plane, scales):
+        def load_scales(rows, scales):
             for q in range(4):
                 nc.sync.dma_start(
-                    out=plane[32 * q : 32 * q + 4, :, :].bitcast(I32),
+                    out=rows[32 * q : 32 * q + 4, :, :].bitcast(I32),
                     in_=scales[:, 4 * q : 4 * q + 4, :].rearrange("a r n -> r a n").bitcast(I32),
                 )
 
         def load_tab(a):
-            tab_w[a] = in_slot(2 * a, [P, T], U32, f"tab_w{a}")
+            tab_w[a] = keep.tile([P, T], U32, name=f"tab_w{a}", align_bytes=64)
             nc.sync.dma_start(
                 out=tab_w[a][:].bitcast(I32),
                 in_=tab_words[a].rearrange("p n i -> p (n i)").bitcast(I32),
             )
 
         def load_w1(a, b):
-            w1_raw[a, b] = in_slot((2 * a + 1, 7 + a)[b], [P, PACK, KP], F32, f"w1_raw{a}{b}")
+            w1_raw[a, b] = on_buffer(f"w1_buf{a}{b}", [P, PACK, KP], F32, f"w1_raw{a}{b}")
             nc.sync.dma_start(
                 out=w1_raw[a, b][:],
                 in_=w1[KP * a : KP * (a + 1), KP * b : KP * (b + 1)].rearrange("(p i) c -> p i c", i=PACK),
             )
 
         def load_w4(b):
-            w4_w[b] = keep.tile([P, 2, KP // 2], I32, name=f"w4_w{b}")
+            w4_w[b] = keep.tile([P, 2, KP // RUN], I32, name=f"w4_w{b}")
             nc.sync.dma_start(
                 out=w4_w[b][:],
                 in_=w4_words[:, :, 2 * KP * b : 2 * KP * (b + 1)].rearrange("a p n -> p a n").bitcast(I32),
@@ -90,7 +102,7 @@ def tile_list_bond_mode_scores_kernel(
             nc.sync.dma_start(out=force_t[s][:], in_=slice_rows(force, s))
 
         def load_page(s):
-            page[s] = in_slot(PAGE_SLOT[s], [P, T2], F32, f"page{s}")
+            page[s] = on_buffer(page_buffer(s), [P, T2], F32, f"page{s}")
             nc.sync.dma_start(out=page[s][:], in_=slice_rows(page0, s))
 
         def load_wgs(t):
@@ -117,35 +129,32 @@ def tile_list_bond_mode_scores_kernel(
         nc.sync.dma_start(idx2[:], offs2)
         force_first = []
         for c, cols in enumerate(HALVES):
-            force_first.append(keep.tile([P, KP], F32, name=f"force_first{c}", tag=f"first{c}", align_bytes=64))
+            force_first.append(keep.tile([P, KP], F32, name=f"force_first{c}"))
             nc.sync.dma_start(out=force_first[c][:], in_=slice_rows(force[:, cols], 0))
         load_force(1)
         load_wgs(0)
-        load_force(2)
         load_page(0)
+        load_force(2)
         nc.sync.dma_start(idx4[:], offs4)
         nc.sync.dma_start(idx3[:], offs3)
         load_wgs(1)
-        load_w1(0, 1)
-        load_chan(0)
-        load_w1(1, 1)
-        load_chan(1)
+        load_page(1)
         load_force(3)
         load_wgs(2)
-        load_page(1)
+        load_w1(0, 1)
+        load_w1(1, 1)
         load_w4(1)
         load_force(4)
         load_wgs(3)
         load_page(2)
-        for s in range(5, NSLICE):
-            load_chan(s - 3)
-            load_force(s)
-        for s in range(5, NSLICE):
+        load_force(5)
+        load_page(3)
+        load_chan(0)
+        load_force(6)
+        load_chan(1)
+        load_force(7)
+        for s in range(2, NSLICE):
             load_chan(s)
-        mode_t = keep.tile([P, NP], F32, name="mode_t")
-        nc.sync.dma_start(out=mode_t[:], in_=mode.partition_broadcast(P))
-        pair_t = in_slot(3, [P, PACK, NP], F32, "pair_t")
-        nc.sync.dma_start(out=pair_t[:], in_=pair.rearrange("(c p) j -> p c j", p=P))
 
         v_w = [keep.tile([P, S], U32, name=f"v_w{a}", align_bytes=64) for a in range(2)]
         v_s = [keep.tile([P, S], U8, name=f"v_s{a}", align_bytes=64) for a in range(2)]
@@ -155,12 +164,14 @@ def tile_list_bond_mode_scores_kernel(
 
         w4_dw, w4_ds = {}, {}
 
-        def deal_w4_words(b):
-            w4_dw[b] = keep.tile([P, 2, PACK, 2 * P], U8, name=f"w4_dw{b}", tag=("w4_dw0", "cast3")[b], align_bytes=64)
-            nc.vector.tensor_copy(out=w4_dw[b][:].bitcast(I32), in_=w4_w[b][:].rearrange("p a (g t) -> p a t g", t=PACK))
+        def deal_w4_words(b, tag):
+            w4_dw[b] = on_buffer(tag, [P, 2, PACK, 2 * P], U8, f"w4_dw{b}")
+            nc.vector.tensor_copy(
+                out=w4_dw[b][:].bitcast(I32), in_=w4_w[b][:].rearrange("p a (g t) -> p a t g", t=PACK)
+            )
 
-        def deal_w4_scales(b):
-            w4_ds[b] = keep.tile([P, 2, PACK, P], U8, name=f"w4_ds{b}", tag=("w4_ds0", "cast2")[b], align_bytes=64)
+        def deal_w4_scales(b, tag):
+            w4_ds[b] = on_buffer(tag, [P, 2, PACK, P], U8, f"w4_ds{b}")
             nc.vector.tensor_copy(
                 out=w4_ds[b][:].rearrange("p a t (g u) -> p a t g u", u=RUN),
                 in_=w4_s[:, :, KP * b : KP * (b + 1)].rearrange("p a (g t u) -> p a t g u", t=PACK, u=RUN),
@@ -169,37 +180,33 @@ def tile_list_bond_mode_scores_kernel(
         w1_q = {}
         w1_s = [keep.tile([P, 2 * KP], U8, name=f"w1_s{b}", align_bytes=64) for b in range(2)]
 
-        def quantize_w1(b, g0, g1, tag):
-            grouped = keep.tile([P, g1 - g0, P // RUN, RUN, PACK], BF16, name=f"w1_bf{b}{g0}", tag=tag, align_bytes=64)
-            if g0 == 0:
-                w1_q[b] = keep.tile([P, 2 * KP], U32, name=f"w1_q{b}", tag=("w1_q0", "placed1")[b], align_bytes=64)
-            step = 2
-            for g in range(g0, g1, step):
-                a, t = divmod(g, PACK)
+        def quantize_w1(b, m0, m1, tag):
+            grouped = on_buffer(tag, [P, m1 - m0, P // RUN, RUN, PACK], BF16, f"w1_bf{b}{m0}")
+            if m0 == 0:
+                w1_q[b] = on_buffer(("w1_q0", "placed1")[b], [P, 2 * KP], U32, f"w1_q{b}")
+            for m in range(m0, m1, 2):
+                a, t = divmod(m, PACK)
                 src = w1_raw[a, b][:].rearrange("p i (g t u) -> p t g u i", t=PACK, u=RUN)
-                nc.scalar.copy(out=grouped[:, g - g0 : g - g0 + step], in_=src[:, t : t + step])
+                nc.scalar.copy(out=grouped[:, m - m0 : m - m0 + 2], in_=src[:, t : t + 2])
             nc.vector.quantize_mx(
-                out=w1_q[b][:, P * g0 : P * g1].bitcast(FP8X4),
-                scales=w1_s[b][:, P * g0 : P * g1],
-                in_=grouped[:].rearrange("p n g u i -> p (n g u i)"),
+                out=w1_q[b][:, P * m0 : P * m1].bitcast(FP8X4),
+                scales=w1_s[b][:, P * m0 : P * m1],
+                in_=grouped[:].rearrange("p m g u i -> p (m g u i)"),
             )
 
-        def gather_words(a, cols):
-            nc.vector.tensor_copy(v_w[a][:, cols], tab_w[a][:].indirect(idx[:, cols.start // 16 : cols.stop // 16]))
-
-        deal_w4_words(0)
-        deal_w4_scales(0)
-        quantize_w1(0, 0, 4, "cast0")
-        quantize_w1(0, 4, 6, "cast1")
+        deal_w4_words(0, "w4_dw0")
+        deal_w4_scales(0, "w4_ds0")
+        quantize_w1(0, 0, 4, "cast_a0")
+        quantize_w1(0, 4, 6, "cast_a1")
         for cols in HALVES:
-            gather_words(1, cols)
-        quantize_w1(0, 6, 8, "cast1")
+            nc.vector.tensor_copy(v_w[1][:, cols], tab_w[1][:].indirect(entries(idx, cols)))
+        quantize_w1(0, 6, 8, "cast_a1")
 
         bend, lin, lin_sb, prod, feat, placed = {}, {}, {}, {}, {}, {}
 
         def products(s):
             b, t = divmod(s, PACK)
-            bend[s] = keep.tile([P, S], F32, name=f"bend{s}", tag=f"bend{s % 4}", align_bytes=64)
+            bend[s] = on_buffer(work_buffer(s), [P, S], F32, f"bend{s}")
             for c, cols in enumerate(HALVES):
                 z = psum.tile([P, KP], F32, name="z", tag="z")
                 lin[s, c] = psum.tile([P, KP], F32, name="y", tag="y")
@@ -218,37 +225,29 @@ def tile_list_bond_mode_scores_kernel(
                         start=(a == 0), stop=(a == 1),
                     )
                 nc.scalar.activation(out=bend[s][:, cols], in_=z[:], func=ACT.Tanh)
-            if s > 2:
-                copy_linear(s)
 
-        def copy_linear(s):
-            if s == 2:
-                lin_sb[s] = keep.tile([P, KP], F32, name="lin_sb2", tag="feat1", align_bytes=64)
-            else:
-                lin_sb[s] = ring.tile([P, KP], F32, name="lin_sb", tag="lin_sb")
-            nc.scalar.copy(out=lin_sb[s][:], in_=lin[s, 1][:])
+        def copy_linear(s, dst):
+            lin_sb[s] = dst
+            nc.scalar.copy(out=dst[:], in_=lin[s, 1][:])
 
-        def times_force(s, cols):
-            if s not in prod:
-                prod[s] = ring.tile([P, S], F32, name="prod", tag="prod", bufs=1)
-            nc.gpsimd.tensor_tensor(out=prod[s][:, cols], in0=bend[s][:, cols], in1=force_t[s][:, cols], op=MULT)
+        def times_force(s):
+            prod[s] = ring.tile([P, S], F32, name="prod", tag="prod", bufs=1)
+            nc.gpsimd.tensor_tensor(out=prod[s][:], in0=bend[s][:], in1=force_t[s][:], op=MULT)
 
         def add_linear(s):
-            tag = {2: "feat0", 3: "cast4"}.get(s, f"bend{(s - 1) % 4}")
-            low = keep.tile([P, KP], F32, name=f"feat_low{s}", tag=tag, align_bytes=64)
+            low = on_buffer(LOW_BUFFER.get(s, work_buffer(s - 1)), [P, KP], F32, f"feat_low{s}")
             nc.vector.tensor_tensor(out=low[:], in0=lin[s, 0][:], in1=prod[s][:, HALVES[0]], op=ADD)
-            high = in_slot(PAGE_SLOT[s - 2], [P, KP], F32, f"feat_high{s}")
+            high = on_buffer(page_buffer(s - 2), [P, KP], F32, f"feat_high{s}")
             nc.gpsimd.tensor_tensor(out=high[:], in0=prod[s][:, HALVES[1]], in1=lin_sb[s][:], op=ADD)
             feat[s] = (low, high)
 
         def weigh(s):
-            placed[s] = keep.tile([P, S], F32, name=f"placed{s}", tag=f"bend{(s + 1) % 4}", align_bytes=64)
+            placed[s] = on_buffer(work_buffer(s + 1), [P, S], F32, f"placed{s}")
             for part, cols in zip(feat[s], HALVES):
                 nc.gpsimd.tensor_tensor(out=placed[s][:, cols], in0=part[:], in1=wg[s % PACK][:, cols], op=MULT)
 
         def scatter(s, cols, values):
-            entries = idx2[:, cols.start // 16 : cols.stop // 16]
-            nc.vector.tensor_copy(page[s][:].indirect(entries), values)
+            nc.vector.tensor_copy(page[s][:].indirect(entries(idx2, cols)), values)
 
         x1_rows, x2_rows, x_g, x_q, x_s = {}, {}, {}, {}, {}
 
@@ -256,17 +255,17 @@ def tile_list_bond_mode_scores_kernel(
             b, t = divmod(s, PACK)
             if t == 0:
                 x1_rows[b] = ring.tile([P, PACK, NP], BF16, name="x1_rows", tag="x1_rows")
-            x2_rows[s] = ring.tile([P, NP], F32, name="x2_rows", tag="x2_rows", bufs=5)
+            x2_rows[s] = ring.tile([P, NP], F32, name="x2_rows", tag="x2_rows", bufs=X2_BUFS)
             nc.vector.tensor_copy(x2_rows[s][:], page[s][:].indirect(idx4[:]))
             nc.vector.tensor_copy(x1_rows[b][:, t, :], page[s][:].indirect(idx3[:]))
 
         def group_x(b):
-            x_g[b] = in_slot(8 - b, [P, 2, NP, PACK], BF16, f"x_g{b}")
+            x_g[b] = on_buffer(f"w1_buf{1 - b}1", [P, 2, NP, PACK], BF16, f"x_g{b}")
             x1_g, x2_g = x_g[b][:, 0], x_g[b][:, 1]
             for t in range(PACK):
                 s = PACK * b + t
                 if b == 0:
-                    mag = in_slot(7, [P, NP], F32, "mag")
+                    mag = on_buffer("w1_buf01", [P, NP], F32, "mag")
                 else:
                     mag = keep.tile([P, NP], F32, name="mag", tag="mag")
                 nc.scalar.activation(out=mag[:], in_=x2_rows[s][:], func=ACT.Abs)
@@ -279,8 +278,8 @@ def tile_list_bond_mode_scores_kernel(
                     else:
                         nc.scalar.copy(out=dst, in_=src)
 
-        def quantize_x(b, pieces):
-            x_q[b] = keep.tile([P, 2 * NP], U32, name=f"x_q{b}", tag=f"bend{3 - b}", align_bytes=64)
+        def quantize_x(b, after, pieces):
+            x_q[b] = on_buffer(work_buffer(after + 1), [P, 2 * NP], U32, f"x_q{b}")
             x_s[b] = keep.tile([P, 2 * NP], U8, name=f"x_s{b}", align_bytes=64)
             for n0, n1 in pieces:
                 nc.vector.quantize_mx(
@@ -289,7 +288,7 @@ def tile_list_bond_mode_scores_kernel(
                 )
 
         products(0)
-        first = [keep.tile([P, KP], F32, name=f"first_feat{c}", tag=f"feat{1 - c}", align_bytes=64) for c in range(2)]
+        first = [on_buffer(f"first_buf{c}", [P, KP], F32, f"first_feat{c}") for c in range(2)]
         for c, cols in enumerate(HALVES):
             nc.vector.tensor_tensor(out=bend[0][:, cols], in0=bend[0][:, cols], in1=force_first[c][:], op=MULT)
         for c, cols in enumerate(HALVES):
@@ -297,42 +296,50 @@ def tile_list_bond_mode_scores_kernel(
             engine = (nc.vector, nc.gpsimd)[c]
             engine.tensor_tensor(out=first[c][:], in0=first[c][:], in1=wg[0][:, cols], op=MULT)
         products(1)
-        prod[1] = bend[1]
         for cols in HALVES:
-            times_force(1, cols)
+            nc.gpsimd.tensor_tensor(out=bend[1][:, cols], in0=bend[1][:, cols], in1=force_t[1][:, cols], op=MULT)
         scatter(0, HALVES[0], first[0][:])
-        second = keep.tile([P, S], F32, name="second_feat", tag="feat1", align_bytes=64)
+        second = on_buffer("first_buf0", [P, S], F32, "second_feat")
         for c, cols in enumerate(HALVES):
             nc.vector.tensor_tensor(out=second[:, cols], in0=lin[1, c][:], in1=bend[1][:, cols], op=ADD)
         scatter(0, HALVES[1], first[1][:])
         products(2)
-        times_force(2, WHOLE)
-        placed[1] = keep.tile([P, S], F32, name="placed1", align_bytes=64)
+        times_force(2)
+        placed[1] = on_buffer("placed1", [P, S], F32, "placed1")
         nc.gpsimd.tensor_tensor(out=placed[1][:], in0=second[:], in1=wg[1][:], op=MULT)
-        copy_linear(2)
+        copy_linear(2, on_buffer("first_buf0", [P, KP], F32, "lin_sb2"))
         fetch(0)
+
         for s in range(1, NSLICE):
             if s + 1 < NSLICE:
                 add_linear(s + 1)
             if s + 2 < NSLICE:
                 products(s + 2)
-                times_force(s + 2, WHOLE)
+                if s + 2 >= PACK:
+                    copy_linear(s + 2, ring.tile([P, KP], F32, name="lin_sb", tag="lin_sb"))
+                times_force(s + 2)
             if s + 1 < NSLICE:
                 weigh(s + 1)
-            if s + 2 < NSLICE:
-                load_page(s + 2)
+            if s + 3 < NSLICE:
+                load_page(s + 3)
+            if s == NSLICE - 3:
+                pair_t = on_buffer(page_buffer(s - 1), [P, PACK, NP], F32, "pair_t")
+                nc.sync.dma_start(out=pair_t[:], in_=pair.rearrange("(c p) j -> p c j", p=P))
+            if s == NSLICE - 2:
+                mode_t = on_buffer(page_buffer(s - 1), [P, NP], F32, "mode_t")
+                nc.sync.dma_start(out=mode_t[:], in_=mode.partition_broadcast(P))
             scatter(s, WHOLE, placed[s][:])
             if s == 1:
-                quantize_w1(1, 0, 4, "cast2")
-                quantize_w1(1, 4, 6, "cast3")
-                quantize_w1(1, 6, 8, "cast4")
-                deal_w4_words(1)
-                deal_w4_scales(1)
+                for n, m in enumerate((0, 4, 2, 6)):
+                    quantize_w1(1, m, m + 2, f"cast_b{n}")
+                copy_linear(3, on_buffer("cast_b2", [P, KP], F32, "lin_sb3"))
+                deal_w4_words(1, "cast_b1")
+                deal_w4_scales(1, "cast_b0")
             fetch(s)
         group_x(0)
-        quantize_x(0, ((0, 2),))
+        quantize_x(0, NSLICE - 2, ((0, 2),))
         group_x(1)
-        quantize_x(1, ((0, 1), (1, 2)))
+        quantize_x(1, NSLICE - 3, ((0, 1), (1, 2)))
 
         e = [psum.tile([P, NP], F32, name="e", tag="z") for c in range(NP // P)]
         for b in range(2):
@@ -344,7 +351,7 @@ def tile_list_bond_mode_scores_kernel(
                     start=(b == 0), stop=(b == 1),
                 )
         for c in range(NP // P):
-            res = ring.tile([P, NP], F32, name="res", tag="x2_rows", bufs=5)
+            res = ring.tile([P, NP], F32, name="res", tag="x2_rows", bufs=X2_BUFS)
             nc.vector.tensor_tensor(out=res[:], in0=e[c][:], in1=pair_t[:, c, :], op=ADD)
             engine = nc.gpsimd if c == 0 else nc.vector
             engine.tensor_tensor(out=res[:], in0=res[:], in1=mode_t[:], op=MULT)

from contextlib import ExitStack

import concourse.mybir as mybir

K, H, T, S, T2, NP = 1024, 1024, 2048, 1024, 2048, 512
FLOPS = 2 * 2 * K * H * S + 2 * H * NP * NP

F32 = mybir.dt.float32
BF16 = mybir.dt.bfloat16
I32 = mybir.dt.int32
U32 = mybir.dt.uint32
U16 = mybir.dt.uint16
U8 = mybir.dt.uint8
FP8X4 = mybir.dt.float8_e4m3fn_x4
FP4X4 = mybir.dt.float4_e2m1fn_x4
MULT = mybir.AluOpType.mult
ADD = mybir.AluOpType.add
ACT = mybir.ActivationFunctionType

P = 128
PACK = 4
RUN = 2
KP = P * PACK
NSLICE = H // P
HALVES = (slice(0, KP), slice(KP, S))
WHOLE = slice(0, S)
PAGE_BUFS = 4
WORK_BUFS = 4
LOW_BUFFER = {2: "first_buf1", 3: "cast_b3"}
X2_BUFS = 5


def tile_list_bond_mode_scores_kernel(
    tc, tab_words, tab_scales, offs, offs2, offs3, offs4, w1, w4_words, w4_scales,
    force, wgs, page0, chan, pair, mode, out,
):
    nc = tc.nc
    with ExitStack() as ctx:
        keep = ctx.enter_context(tc.tile_pool(name="keep", bufs=1))
        ring = ctx.enter_context(tc.tile_pool(name="ring", bufs=2))
        psum = ctx.enter_context(tc.psum_pool(name="psum", bufs=4))

        def on_buffer(tag, shape, dtype, name):
            return keep.tile(shape, dtype, name=name, tag=tag, align_bytes=64)

        def page_buffer(s):
            return f"page_buf{s % PAGE_BUFS}"

        def work_buffer(n):
            return f"work_buf{n % WORK_BUFS}"

        def slice_rows(mat, s):
            b, t = divmod(s, PACK)
            return mat[KP * b : KP * (b + 1), :].rearrange("(g t u) j -> t g u j", t=PACK, u=RUN)[t]

        def entries(offsets, cols):
            return offsets[:, cols.start // 16 : cols.stop // 16]

        idx = keep.tile([P, S // 16], U16, name="idx")
        idx2 = keep.tile([P, S // 16], U16, name="idx2")
        idx3 = keep.tile([P, NP // 16], U16, name="idx3")
        idx4 = keep.tile([P, NP // 16], U16, name="idx4")

        tab_s = keep.tile([P, 2, T], U8, name="tab_s", align_bytes=64)
        w4_s = keep.tile([P, 2, H], U8, name="w4_s", align_bytes=64)
        nc.gpsimd.memset(tab_s[:, 0, :].bitcast(I32), 0)
        nc.vector.memset(tab_s[:, 1, :].bitcast(I32), 0)
        nc.vector.memset(w4_s[:].rearrange("p a n -> p (a n)").bitcast(I32), 0)

        tab_w, w1_raw, w4_w, force_t, page, wg, chan_t = {}, {}, {}, {}, {}, {}, {}

        def load_scales(rows, scales):
            for q in range(4):
                nc.sync.dma_start(
                    out=rows[32 * q : 32 * q + 4, :, :].bitcast(I32),
                    in_=scales[:, 4 * q : 4 * q + 4, :].rearrange("a r n -> r a n").bitcast(I32),
                )

        def load_tab(a):
            tab_w[a] = keep.tile([P, T], U32, name=f"tab_w{a}", align_bytes=64)
            nc.sync.dma_start(
                out=tab_w[a][:].bitcast(I32),
                in_=tab_words[a].rearrange("p n i -> p (n i)").bitcast(I32),
            )

        def load_w1(a, b):
            w1_raw[a, b] = on_buffer(f"w1_buf{a}{b}", [P, PACK, KP], F32, f"w1_raw{a}{b}")
            nc.sync.dma_start(
                out=w1_raw[a, b][:],
                in_=w1[KP * a : KP * (a + 1), KP * b : KP * (b + 1)].rearrange("(p i) c -> p i c", i=PACK),
            )

        def load_w4(b):
            w4_w[b] = keep.tile([P, 2, KP // RUN], I32, name=f"w4_w{b}")
            nc.sync.dma_start(
                out=w4_w[b][:],
                in_=w4_words[:, :, 2 * KP * b : 2 * KP * (b + 1)].rearrange("a p n -> p a n").bitcast(I32),
            )

        def load_force(s):
            force_t[s] = keep.tile([P, S], F32, name=f"force{s}")
            nc.sync.dma_start(out=force_t[s][:], in_=slice_rows(force, s))

        def load_page(s):
            page[s] = on_buffer(page_buffer(s), [P, T2], F32, f"page{s}")
            nc.sync.dma_start(out=page[s][:], in_=slice_rows(page0, s))

        def load_wgs(t):
            wg[t] = keep.tile([P, S], F32, name=f"wg{t}")
            for q in (0, 2, 1, 3):
                nc.sync.dma_start(
                    out=wg[t][32 * q : 32 * (q + 1), :],
                    in_=wgs.rearrange("(g t u) j -> t g u j", t=PACK, u=RUN)[t],
                )

        def load_chan(s):
            chan_t[s] = keep.tile([P, 1], F32, name=f"chan{s}")
            with nc.allow_non_contiguous_dma(reason="one value a partition"):
                nc.sync.dma_start(out=chan_t[s][:], in_=slice_rows(chan.unsqueeze(1), s))

        nc.sync.dma_start(idx[:], offs)
        load_w4(0)
        load_scales(tab_s, tab_scales)
        load_w1(0, 0)
        load_tab(0)
        load_scales(w4_s, w4_scales)
        load_w1(1, 0)
        load_tab(1)
        nc.sync.dma_start(idx2[:], offs2)
        force_first = []
        for c, cols in enumerate(HALVES):
            force_first.append(keep.tile([P, KP], F32, name=f"force_first{c}"))
            nc.sync.dma_start(out=force_first[c][:], in_=slice_rows(force[:, cols], 0))
        load_force(1)
        load_wgs(0)
        load_page(0)
        load_force(2)
        nc.sync.dma_start(idx4[:], offs4)
        nc.sync.dma_start(idx3[:], offs3)
        load_wgs(1)
        load_page(1)
        load_force(3)
        load_wgs(2)
        load_w1(0, 1)
        load_w1(1, 1)
        load_w4(1)
        load_force(4)
        load_wgs(3)
        load_page(2)
        load_force(5)
        load_page(3)
        load_chan(0)
        load_force(6)
        load_chan(1)
        load_force(7)
        for s in range(2, NSLICE):
            load_chan(s)

        v_w = [keep.tile([P, S], U32, name=f"v_w{a}", align_bytes=64) for a in range(2)]
        v_s = [keep.tile([P, S], U8, name=f"v_s{a}", align_bytes=64) for a in range(2)]
        for a in range(2):
            nc.vector.tensor_copy(v_s[a][:], tab_s[:, a, :].indirect(idx[:]))
        nc.vector.tensor_copy(v_w[0][:], tab_w[0][:].indirect(idx[:]))

        w4_dw, w4_ds = {}, {}

        def deal_w4_words(b, tag):
            w4_dw[b] = on_buffer(tag, [P, 2, PACK, 2 * P], U8, f"w4_dw{b}")
            nc.vector.tensor_copy(
                out=w4_dw[b][:].bitcast(I32), in_=w4_w[b][:].rearrange("p a (g t) -> p a t g", t=PACK)
            )

        def deal_w4_scales(b, tag):
            w4_ds[b] = on_buffer(tag, [P, 2, PACK, P], U8, f"w4_ds{b}")
            nc.vector.tensor_copy(
                out=w4_ds[b][:].rearrange("p a t (g u) -> p a t g u", u=RUN),
                in_=w4_s[:, :, KP * b : KP * (b + 1)].rearrange("p a (g t u) -> p a t g u", t=PACK, u=RUN),
            )

        w1_q = {}
        w1_s = [keep.tile([P, 2 * KP], U8, name=f"w1_s{b}", align_bytes=64) for b in range(2)]

        def quantize_w1(b, m0, m1, tag):
            grouped = on_buffer(tag, [P, m1 - m0, P // RUN, RUN, PACK], BF16, f"w1_bf{b}{m0}")
            if m0 == 0:
                w1_q[b] = on_buffer(("w1_q0", "placed1")[b], [P, 2 * KP], U32, f"w1_q{b}")
            for m in range(m0, m1, 2):
                a, t = divmod(m, PACK)
                src = w1_raw[a, b][:].rearrange("p i (g t u) -> p t g u i", t=PACK, u=RUN)
                nc.scalar.copy(out=grouped[:, m - m0 : m - m0 + 2], in_=src[:, t : t + 2])
            nc.vector.quantize_mx(
                out=w1_q[b][:, P * m0 : P * m1].bitcast(FP8X4),
                scales=w1_s[b][:, P * m0 : P * m1],
                in_=grouped[:].rearrange("p m g u i -> p (m g u i)"),
            )

        deal_w4_words(0, "w4_dw0")
        deal_w4_scales(0, "w4_ds0")
        quantize_w1(0, 0, 4, "cast_a0")
        quantize_w1(0, 4, 6, "cast_a1")
        for cols in HALVES:
            nc.vector.tensor_copy(v_w[1][:, cols], tab_w[1][:].indirect(entries(idx, cols)))
        quantize_w1(0, 6, 8, "cast_a1")

        bend, lin, lin_sb, prod, feat, placed = {}, {}, {}, {}, {}, {}

        def products(s):
            b, t = divmod(s, PACK)
            bend[s] = on_buffer(work_buffer(s), [P, S], F32, f"bend{s}")
            for c, cols in enumerate(HALVES):
                z = psum.tile([P, KP], F32, name="z", tag="z")
                lin[s, c] = psum.tile([P, KP], F32, name="y", tag="y")
                for a in range(2):
                    rows = slice(KP * a + P * t, KP * a + P * (t + 1))
                    nc.tensor.matmul_mx(
                        out=z[:], lhsT=w1_q[b][:, rows].bitcast(FP8X4), lhsT_scale=w1_s[b][:, rows],
                        rhs=v_w[a][:, cols].bitcast(FP8X4), rhs_scale=v_s[a][:, cols],
                        start=(a == 0), stop=(a == 1),
                    )
                for a in range(2):
                    nc.tensor.matmul_mx(
                        out=lin[s, c][:], lhsT=w4_dw[b][:, a, t, :].bitcast(FP4X4),
                        lhsT_scale=w4_ds[b][:, a, t, :],
                        rhs=v_w[a][:, cols].bitcast(FP8X4), rhs_scale=v_s[a][:, cols],
                        start=(a == 0), stop=(a == 1),
                    )
                nc.scalar.activation(out=bend[s][:, cols], in_=z[:], func=ACT.Tanh)

        def copy_linear(s, dst):
            lin_sb[s] = dst
            nc.scalar.copy(out=dst[:], in_=lin[s, 1][:])

        def times_force(s):
            prod[s] = ring.tile([P, S], F32, name="prod", tag="prod", bufs=1)
            nc.gpsimd.tensor_tensor(out=prod[s][:], in0=bend[s][:], in1=force_t[s][:], op=MULT)

        def add_linear(s):
            low = on_buffer(LOW_BUFFER.get(s, work_buffer(s - 1)), [P, KP], F32, f"feat_low{s}")
            nc.vector.tensor_tensor(out=low[:], in0=lin[s, 0][:], in1=prod[s][:, HALVES[0]], op=ADD)
            high = on_buffer(page_buffer(s - 2), [P, KP], F32, f"feat_high{s}")
            nc.gpsimd.tensor_tensor(out=high[:], in0=prod[s][:, HALVES[1]], in1=lin_sb[s][:], op=ADD)
            feat[s] = (low, high)

        def weigh(s):
            placed[s] = on_buffer(work_buffer(s + 1), [P, S], F32, f"placed{s}")
            for part, cols in zip(feat[s], HALVES):
                nc.gpsimd.tensor_tensor(out=placed[s][:, cols], in0=part[:], in1=wg[s % PACK][:, cols], op=MULT)

        def scatter(s, cols, values):
            nc.vector.tensor_copy(page[s][:].indirect(entries(idx2, cols)), values)

        x1_rows, x2_rows, x_g, x_q, x_s = {}, {}, {}, {}, {}

        def fetch(s):
            b, t = divmod(s, PACK)
            if t == 0:
                x1_rows[b] = ring.tile([P, PACK, NP], BF16, name="x1_rows", tag="x1_rows")
            x2_rows[s] = ring.tile([P, NP], F32, name="x2_rows", tag="x2_rows", bufs=X2_BUFS)
            nc.vector.tensor_copy(x2_rows[s][:], page[s][:].indirect(idx4[:]))
            nc.vector.tensor_copy(x1_rows[b][:, t, :], page[s][:].indirect(idx3[:]))

        def group_x(b):
            x_g[b] = on_buffer(f"w1_buf{1 - b}1", [P, 2, NP, PACK], BF16, f"x_g{b}")
            x1_g, x2_g = x_g[b][:, 0], x_g[b][:, 1]
            for t in range(PACK):
                s = PACK * b + t
                if b == 0:
                    mag = on_buffer("w1_buf01", [P, NP], F32, "mag")
                else:
                    mag = keep.tile([P, NP], F32, name="mag", tag="mag")
                nc.scalar.activation(out=mag[:], in_=x2_rows[s][:], func=ACT.Abs)
                nc.scalar.activation(out=x2_g[:, :, t], in_=mag[:], func=ACT.Copy, scale=chan_t[s][:])
                if t % 2 == 1:
                    dst = x1_g[:, :, t - 1 : t + 1]
                    src = x1_rows[b][:, t - 1 : t + 1, :].rearrange("p t m -> p m t")
                    if s == NSLICE - 1:
                        nc.vector.tensor_copy(out=dst, in_=src)
                    else:
                        nc.scalar.copy(out=dst, in_=src)

        def quantize_x(b, after, pieces):
            x_q[b] = on_buffer(work_buffer(after + 1), [P, 2 * NP], U32, f"x_q{b}")
            x_s[b] = keep.tile([P, 2 * NP], U8, name=f"x_s{b}", align_bytes=64)
            for n0, n1 in pieces:
                nc.vector.quantize_mx(
                    out=x_q[b][:, NP * n0 : NP * n1].bitcast(FP8X4), scales=x_s[b][:, NP * n0 : NP * n1],
                    in_=x_g[b][:, n0:n1].rearrange("p n m t -> p (n m t)"),
                )

        products(0)
        first = [on_buffer(f"first_buf{c}", [P, KP], F32, f"first_feat{c}") for c in range(2)]
        for c, cols in enumerate(HALVES):
            nc.vector.tensor_tensor(out=bend[0][:, cols], in0=bend[0][:, cols], in1=force_first[c][:], op=MULT)
        for c, cols in enumerate(HALVES):
            nc.vector.tensor_tensor(out=first[c][:], in0=lin[0, c][:], in1=bend[0][:, cols], op=ADD)
            engine = (nc.vector, nc.gpsimd)[c]
            engine.tensor_tensor(out=first[c][:], in0=first[c][:], in1=wg[0][:, cols], op=MULT)
        products(1)
        for cols in HALVES:
            nc.gpsimd.tensor_tensor(out=bend[1][:, cols], in0=bend[1][:, cols], in1=force_t[1][:, cols], op=MULT)
        scatter(0, HALVES[0], first[0][:])
        second = on_buffer("first_buf0", [P, S], F32, "second_feat")
        for c, cols in enumerate(HALVES):
            nc.vector.tensor_tensor(out=second[:, cols], in0=lin[1, c][:], in1=bend[1][:, cols], op=ADD)
        scatter(0, HALVES[1], first[1][:])
        products(2)
        times_force(2)
        placed[1] = on_buffer("placed1", [P, S], F32, "placed1")
        nc.gpsimd.tensor_tensor(out=placed[1][:], in0=second[:], in1=wg[1][:], op=MULT)
        copy_linear(2, on_buffer("first_buf0", [P, KP], F32, "lin_sb2"))
        fetch(0)

        for s in range(1, NSLICE):
            if s + 1 < NSLICE:
                add_linear(s + 1)
            if s + 2 < NSLICE:
                products(s + 2)
                if s + 2 >= PACK:
                    copy_linear(s + 2, ring.tile([P, KP], F32, name="lin_sb", tag="lin_sb"))
                times_force(s + 2)
            if s + 1 < NSLICE:
                weigh(s + 1)
            if s + 3 < NSLICE:
                load_page(s + 3)
            if s == NSLICE - 3:
                pair_t = on_buffer(page_buffer(s - 1), [P, PACK, NP], F32, "pair_t")
                nc.sync.dma_start(out=pair_t[:], in_=pair.rearrange("(c p) j -> p c j", p=P))
            if s == NSLICE - 2:
                mode_t = on_buffer(page_buffer(s - 1), [P, NP], F32, "mode_t")
                nc.sync.dma_start(out=mode_t[:], in_=mode.partition_broadcast(P))
            scatter(s, WHOLE, placed[s][:])
            if s == 1:
                for n, m in enumerate((0, 4, 2, 6)):
                    quantize_w1(1, m, m + 2, f"cast_b{n}")
                copy_linear(3, on_buffer("cast_b2", [P, KP], F32, "lin_sb3"))
                deal_w4_words(1, "cast_b1")
                deal_w4_scales(1, "cast_b0")
            fetch(s)
        group_x(0)
        quantize_x(0, NSLICE - 2, ((0, 2),))
        group_x(1)
        quantize_x(1, NSLICE - 3, ((0, 1), (1, 2)))

        e = [psum.tile([P, NP], F32, name="e", tag="z") for c in range(NP // P)]
        for b in range(2):
            for c in range(NP // P):
                cols = slice(c * P, (c + 1) * P)
                nc.tensor.matmul_mx(
                    out=e[c][:], lhsT=x_q[b][:, cols].bitcast(FP8X4), lhsT_scale=x_s[b][:, cols],
                    rhs=x_q[b][:, NP:].bitcast(FP8X4), rhs_scale=x_s[b][:, NP:],
                    start=(b == 0), stop=(b == 1),
                )
        for c in range(NP // P):
            res = ring.tile([P, NP], F32, name="res", tag="x2_rows", bufs=X2_BUFS)
            nc.vector.tensor_tensor(out=res[:], in0=e[c][:], in1=pair_t[:, c, :], op=ADD)
            engine = nc.gpsimd if c == 0 else nc.vector
            engine.tensor_tensor(out=res[:], in0=res[:], in1=mode_t[:], op=MULT)
            nc.sync.dma_start(out=out[c * P : (c + 1) * P, :], in_=res[:])
